import numpy as np
import ml_dtypes


def mxq(x, axis, fmt="e4m3"):
    dtype, down = {"e4m3": (ml_dtypes.float8_e4m3fn, 7), "e5m2": (ml_dtypes.float8_e5m2, 14)}[fmt]
    v = np.moveaxis(np.asarray(x, np.float32).astype(ml_dtypes.bfloat16).astype(np.float64), axis, -1)
    blocks = v.reshape(v.shape[:-1] + (-1, 32))
    amax = np.abs(blocks).max(-1, keepdims=True)
    byte = np.maximum(np.where(amax > 0, np.frexp(amax)[1] - 1 + 127, 0) - down, 1)
    scale = np.exp2(byte - 127.0)
    codes = (blocks / scale).astype(np.float32).astype(dtype).astype(np.float64)
    return np.moveaxis((codes * scale).reshape(v.shape), -1, axis)


WIDE = False


def mx_kscale(k):
    if not WIDE:
        return np.ones(k)
    levels = np.array([10, -10, 5, -5, 0])
    if k % 512:
        return np.exp2(np.random.permutation(np.resize(levels, k // 32))).repeat(32)
    a = np.empty((k // 512, 16))
    for p in range(k // 512):
        a[p, :8] = np.random.permutation(np.resize(levels, 8))
        for g in range(8):
            far = levels[np.abs(levels - a[p, g]) >= 10]
            a[p, g + 8] = far[np.random.randint(len(far))]
    return np.exp2(a.ravel()).repeat(32)


def f64(x):
    return np.asarray(x).astype(np.float64)


def striped(idx):
    return np.tile(idx.reshape(-1, 16).T, (8, 1)).astype(np.uint16)


def unstriped(offs):
    return offs[:16].T.reshape(-1).astype(np.int64)


K, T, E, C, N = 1024, 2048, 8, 256, 128


def by_expert(wq, xq):
    return np.concatenate([wq[e].T @ xq[:, e * C:(e + 1) * C] for e in range(E)], axis=1)


def setup_inputs():
    n = np.random.standard_normal
    s = mx_kscale(K)[:, None]
    return {
        "xT": (n((K, T)) * s).astype(np.float32),
        "w": (n((E, K, N)) / np.sqrt(K) / s[None]).astype(np.float32),
        "gate": np.tile(np.random.uniform(0.2, 1.0, E * C), (N, 1)).astype(np.float32),
        "offs": striped(np.random.permutation(T)[:E * C]),
    }


def reference(xT, w, gate, offs):
    idx = unstriped(offs)
    xq = mxq(f64(xT)[:, idx], 0, "e4m3")
    y = by_expert(mxq(f64(w), 1, "e4m3"), xq)
    out = np.zeros((N, T))
    out[:, idx] = f64(gate) * y
    return out

@@ -1,0 +1,140 @@
+from contextlib import ExitStack
+
+import concourse.mybir as mybir
+
+K, T, E, C, N = 1024, 2048, 8, 256, 128
+FLOPS = 2 * K * N * E * C
+
+F32 = mybir.dt.float32
+BF16 = mybir.dt.bfloat16
+U32 = mybir.dt.uint32
+U16 = mybir.dt.uint16
+U8 = mybir.dt.uint8
+FP8X4 = mybir.dt.float8_e4m3fn_x4
+MULT = mybir.AluOpType.mult
+
+P = 128
+PACK = 4
+PASSES = K // (P * PACK)
+SLOTS = E * C
+SUB = 512
+W_EXPERTS = 4
+
+
+def tile_routed_moe_kernel(tc, xT, w, gate, offs, out):
+    nc = tc.nc
+    x_planes = xT.rearrange("(g p t) n -> g p t n", g=PASSES, p=P, t=PACK)
+    w_rows = w.rearrange("e (g p t) n -> g p e (t n)", g=PASSES, p=P, t=PACK)
+
+    with ExitStack() as ctx:
+        keep = ctx.enter_context(tc.tile_pool(name="keep", bufs=1))
+        gpool = ctx.enter_context(tc.tile_pool(name="gpool", bufs=3))
+        ipool = ctx.enter_context(tc.tile_pool(name="ipool", bufs=4))
+        wpool = ctx.enter_context(tc.tile_pool(name="wpool", bufs=2))
+        psum = ctx.enter_context(tc.psum_pool(name="psum", bufs=1))
+
+        offsets = keep.tile([P, SLOTS // 16], U16, name="offsets")
+        nc.sync.dma_start(offsets[:], offs)
+
+        planes = [[keep.tile([P, T], F32, name="plane%d%d" % (g, t)) for t in range(PACK)] for g in range(PASSES)]
+        w_raw = [[keep.tile([P, W_EXPERTS, PACK * N], F32, name="wraw%d%d" % (g, h)) for h in range(E // W_EXPERTS)] for g in range(PASSES)]
+        gate_sb = keep.tile([P, SLOTS], F32, name="gate_sb")
+
+        def load_plane(g, t):
+            nc.sync.dma_start(out=planes[g][t][:], in_=x_planes[g, :, t, :])
+
+        def load_w(g, h):
+            nc.sync.dma_start(out=w_raw[g][h][:], in_=w_rows[g, :, h * W_EXPERTS:(h + 1) * W_EXPERTS, :])
+
+        load_plane(0, 0)
+        load_plane(0, 1)
+        load_w(0, 0)
+        load_plane(0, 2)
+        load_w(0, 1)
+        load_plane(0, 3)
+        load_plane(1, 0)
+        load_plane(1, 1)
+        load_plane(1, 2)
+        load_w(1, 0)
+        load_plane(1, 3)
+        load_w(1, 1)
+        nc.sync.dma_start(out=gate_sb[:], in_=gate)
+
+        x_codes = keep.tile([P, PASSES, SLOTS], U32, name="x_codes", align_bytes=64)
+        x_scales = keep.tile([P, PASSES, SLOTS], U8, name="x_scales", align_bytes=64)
+        w_codes = keep.tile([P, PASSES, E * N], U32, name="w_codes", align_bytes=64)
+        w_scales = keep.tile([P, PASSES, E * N], U8, name="w_scales", align_bytes=64)
+        window = keep.tile([P, T], F32, name="window")
+
+        def gather(g, t, dst, first, count):
+            nc.vector.tensor_copy(dst[:, t, :], planes[g][t][:].indirect(offsets[:, first // 16:(first + count) // 16]))
+
+        def quantize_slots(g, src, src_first, first):
+            grouped = ipool.tile([P, SUB, PACK], BF16, name="grouped", align_bytes=64)
+            nc.scalar.copy(out=grouped[:], in_=src[:, :, src_first:src_first + SUB].rearrange("p t n -> p n t"))
+            nc.vector.quantize_mx(
+                out=x_codes[:, g, first:first + SUB].bitcast(FP8X4),
+                scales=x_scales[:, g, first:first + SUB],
+                in_=grouped[:].rearrange("p n t -> p (n t)"),
+            )
+
+        def quantize_w(g, h):
+            w_grouped = wpool.tile([P, W_EXPERTS, N, PACK], BF16, name="w_grouped", align_bytes=64)
+            nc.scalar.copy(out=w_grouped[:], in_=w_raw[g][h][:].rearrange("p e (t n) -> p e n t", t=PACK))
+            cols = slice(h * W_EXPERTS * N, (h + 1) * W_EXPERTS * N)
+            nc.vector.quantize_mx(
+                out=w_codes[:, g, cols].bitcast(FP8X4),
+                scales=w_scales[:, g, cols],
+                in_=w_grouped[:].rearrange("p e n t -> p (e n t)"),
+            )
+
+        half = SLOTS // 2
+        g0 = [gpool.tile([P, PACK, half], F32, name="g4") for h in range(2)]
+        for t in range(PACK):
+            for h in range(2):
+                gather(0, t, g0[h], h * half, half)
+            if t == 1:
+                quantize_w(0, 0)
+            if t == 2:
+                quantize_w(0, 1)
+        for h in range(2):
+            for s in range(half // SUB):
+                quantize_slots(0, g0[h], s * SUB, h * half + s * SUB)
+
+        sums = []
+        first = 0
+        for ci, count in enumerate((1024, 512, 512)):
+            g1 = gpool.tile([P, PACK, count], F32, name="g4")
+            for t in range(PACK):
+                gather(1, t, g1, first, count)
+            if ci < 2:
+                quantize_w(1, ci)
+            for s in range(count // SUB):
+                lo = first + s * SUB
+                quantize_slots(1, g1, s * SUB, lo)
+                acc = psum.tile([P, SUB], F32, name="acc%d" % (lo // SUB))
+                for j in range(SUB // C):
+                    e = lo // C + j
+                    for g in range(PASSES):
+                        nc.tensor.matmul_mx(
+                            out=acc[:, j * C:(j + 1) * C],
+                            lhsT=w_codes[:, g, e * N:(e + 1) * N].bitcast(FP8X4),
+                            lhsT_scale=w_scales[:, g, e * N:(e + 1) * N],
+                            rhs=x_codes[:, g, e * C:(e + 1) * C].bitcast(FP8X4),
+                            rhs_scale=x_scales[:, g, e * C:(e + 1) * C],
+                            start=(g == 0),
+                            stop=(g == PASSES - 1),
+                        )
+                y = keep.tile([P, SUB], F32, name="y%d" % (lo // SUB))
+                nc.scalar.copy(out=y[:], in_=acc[:])
+                sums.append((lo, y))
+            first += count
+
+        for lo, y in sums:
+            nc.vector.tensor_tensor(
+                window[:].indirect(offsets[:, lo // 16:(lo + SUB) // 16]),
+                y[:],
+                gate_sb[:, lo:lo + SUB],
+                MULT,
+            )
+        nc.sync.dma_start(out=out, in_=window[:])

@@ -12,6 +12,7 @@ U16 = mybir.dt.uint16
 U8 = mybir.dt.uint8
 FP8X4 = mybir.dt.float8_e4m3fn_x4
 MULT = mybir.AluOpType.mult
+COPY = mybir.ActivationFunctionType.Copy
 
 P = 128
 PACK = 4
@@ -19,6 +20,8 @@ PASSES = K // (P * PACK)
 SLOTS = E * C
 SUB = 512
 W_EXPERTS = 4
+VPLANES = 3
+CHUNKS = (((0, 1024), (1024, 1024)), ((0, 1024), (1024, 512), (1536, 512)))
 
 
 def tile_routed_moe_kernel(tc, xT, w, gate, offs, out):
@@ -28,113 +31,219 @@ def tile_routed_moe_kernel(tc, xT, w, gate, offs, out):
 
     with ExitStack() as ctx:
         keep = ctx.enter_context(tc.tile_pool(name="keep", bufs=1))
-        gpool = ctx.enter_context(tc.tile_pool(name="gpool", bufs=3))
-        ipool = ctx.enter_context(tc.tile_pool(name="ipool", bufs=4))
-        wpool = ctx.enter_context(tc.tile_pool(name="wpool", bufs=2))
+        stage = ctx.enter_context(tc.tile_pool(name="stage", bufs=8))
+        late_p = ctx.enter_context(tc.tile_pool(name="late_p", bufs=1))
+        late_a = ctx.enter_context(tc.tile_pool(name="late_a", bufs=1))
+        late_g = ctx.enter_context(tc.tile_pool(name="late_g", bufs=1))
         psum = ctx.enter_context(tc.psum_pool(name="psum", bufs=1))
 
         offsets = keep.tile([P, SLOTS // 16], U16, name="offsets")
         nc.sync.dma_start(offsets[:], offs)
 
-        planes = [[keep.tile([P, T], F32, name="plane%d%d" % (g, t)) for t in range(PACK)] for g in range(PASSES)]
-        w_raw = [[keep.tile([P, W_EXPERTS, PACK * N], F32, name="wraw%d%d" % (g, h)) for h in range(E // W_EXPERTS)] for g in range(PASSES)]
+        planes = {}
+        w_raw = {}
+        w_grouped = {}
+        grouped = {}
+        gathered = {}
+        scales = {}
+        acc = {}
+        sums = {}
         gate_sb = keep.tile([P, SLOTS], F32, name="gate_sb")
 
         def load_plane(g, t):
-            nc.sync.dma_start(out=planes[g][t][:], in_=x_planes[g, :, t, :])
+            if (g, t) == (1, VPLANES - 1):
+                raw = late_p.tile([P, T], F32, name="last_plane", offset=0)
+            else:
+                raw = stage.tile([P, T], F32, name="raw")
+            nc.sync.dma_start(out=raw[:], in_=x_planes[g, :, t, :])
+            planes[(g, t)] = raw
 
         def load_w(g, h):
-            nc.sync.dma_start(out=w_raw[g][h][:], in_=w_rows[g, :, h * W_EXPERTS:(h + 1) * W_EXPERTS, :])
+            raw = stage.tile([P, W_EXPERTS, PACK * N], F32, name="raw")
+            nc.sync.dma_start(out=raw[:], in_=w_rows[g, :, h * W_EXPERTS:(h + 1) * W_EXPERTS, :])
+            w_raw[(g, h)] = raw
 
         load_plane(0, 0)
-        load_plane(0, 1)
-        load_w(0, 0)
-        load_plane(0, 2)
-        load_w(0, 1)
         load_plane(0, 3)
-        load_plane(1, 0)
-        load_plane(1, 1)
-        load_plane(1, 2)
-        load_w(1, 0)
+        load_plane(0, 1)
         load_plane(1, 3)
+        load_plane(0, 2)
+        load_w(0, 0)
+        load_plane(1, 0)
+        load_w(1, 0)
+        load_plane(1, 1)
+        load_w(0, 1)
         load_w(1, 1)
+        load_plane(1, 2)
         nc.sync.dma_start(out=gate_sb[:], in_=gate)
 
         x_codes = keep.tile([P, PASSES, SLOTS], U32, name="x_codes", align_bytes=64)
-        x_scales = keep.tile([P, PASSES, SLOTS], U8, name="x_scales", align_bytes=64)
         w_codes = keep.tile([P, PASSES, E * N], U32, name="w_codes", align_bytes=64)
-        w_scales = keep.tile([P, PASSES, E * N], U8, name="w_scales", align_bytes=64)
         window = keep.tile([P, T], F32, name="window")
+        xb = keep.tile([P, PASSES, T], BF16, name="xb")
 
-        def gather(g, t, dst, first, count):
-            nc.vector.tensor_copy(dst[:, t, :], planes[g][t][:].indirect(offsets[:, first // 16:(first + count) // 16]))
+        def scale_tiles():
+            if not scales:
+                scales["x"] = late_p.tile([P, PASSES, SLOTS], U8, name="x_scales", offset=0, align_bytes=64)
+                scales["w"] = late_p.tile([P, PASSES, E * N], U8, name="w_scales", offset=PASSES * SLOTS, align_bytes=64)
+            return scales
 
-        def quantize_slots(g, src, src_first, first):
-            grouped = ipool.tile([P, SUB, PACK], BF16, name="grouped", align_bytes=64)
-            nc.scalar.copy(out=grouped[:], in_=src[:, :, src_first:src_first + SUB].rearrange("p t n -> p n t"))
-            nc.vector.quantize_mx(
-                out=x_codes[:, g, first:first + SUB].bitcast(FP8X4),
-                scales=x_scales[:, g, first:first + SUB],
-                in_=grouped[:].rearrange("p n t -> p (n t)"),
+        def gathered_tile(g, i):
+            if (g, i) not in gathered:
+                shape = [P, VPLANES, CHUNKS[g][i][1]]
+                if (g, i) == (1, 0):
+                    gathered[(g, i)] = late_a.tile(shape, F32, name="gathered1_0", offset=0)
+                else:
+                    gathered[(g, i)] = keep.tile(shape, F32, name="gathered%d_%d" % (g, i))
+            return gathered[(g, i)]
+
+        def grouped_tile(g, s):
+            if (g, s) not in grouped:
+                shape = [P, SUB, PACK]
+                if (g, s) == (1, 2):
+                    grouped[(g, s)] = late_a.tile(shape, BF16, name="grouped1_2", offset=8192, align_bytes=64)
+                elif (g, s) in ((1, 0), (1, 3)):
+                    grouped[(g, s)] = late_g.tile(shape, BF16, name="grouped1_%d" % s, offset=0, align_bytes=64)
+                else:
+                    grouped[(g, s)] = keep.tile(shape, BF16, name="grouped%d_%d" % (g, s), align_bytes=64)
+            return grouped[(g, s)]
+
+        def gather_v(g, t, i):
+            first, count = CHUNKS[g][i]
+            nc.vector.tensor_copy(gathered_tile(g, i)[:, t, :], planes[(g, t)][:].indirect(offsets[:, first // 16:(first + count) // 16]))
+
+        def gather_s(g, s):
+            nc.scalar.activation(
+                out=grouped_tile(g, s)[:, :, VPLANES],
+                in_=xb[:, g, :].indirect(offsets[:, s * SUB // 16:(s + 1) * SUB // 16]),
+                func=COPY,
             )
 
+        def interleave(g, s):
+            i = [j for j, (first, count) in enumerate(CHUNKS[g]) if first <= s * SUB < first + count][0]
+            src = gathered_tile(g, i)
+            lo = s * SUB - CHUNKS[g][i][0]
+            nc.scalar.copy(out=grouped_tile(g, s)[:, :, 0:VPLANES], in_=src[:, :, lo:lo + SUB].rearrange("p t n -> p n t"))
+
+        def quantize_slots(g, s):
+            nc.vector.quantize_mx(
+                out=x_codes[:, g, s * SUB:(s + 1) * SUB].bitcast(FP8X4),
+                scales=scale_tiles()["x"][:, g, s * SUB:(s + 1) * SUB],
+                in_=grouped_tile(g, s)[:].rearrange("p n t -> p (n t)"),
+            )
+
+        def interleave_w(g, h, engine):
+            shape = [P, W_EXPERTS, N, PACK]
+            if h == 1:
+                wg = late_a.tile(shape, BF16, name="w_grouped%d1" % g, offset=4096 * g, align_bytes=64)
+            else:
+                wg = keep.tile(shape, BF16, name="w_grouped%d0" % g, align_bytes=64)
+            src = w_raw[(g, h)][:].rearrange("p e (t n) -> p e n t", t=PACK)
+            if engine == "V":
+                nc.vector.tensor_copy(out=wg[:], in_=src)
+            elif engine == "G":
+                for e in range(W_EXPERTS):
+                    nc.gpsimd.tensor_copy(out=wg[:, e], in_=src[:, e])
+            else:
+                nc.scalar.copy(out=wg[:], in_=src)
+            w_grouped[(g, h)] = wg
+
         def quantize_w(g, h):
-            w_grouped = wpool.tile([P, W_EXPERTS, N, PACK], BF16, name="w_grouped", align_bytes=64)
-            nc.scalar.copy(out=w_grouped[:], in_=w_raw[g][h][:].rearrange("p e (t n) -> p e n t", t=PACK))
             cols = slice(h * W_EXPERTS * N, (h + 1) * W_EXPERTS * N)
             nc.vector.quantize_mx(
                 out=w_codes[:, g, cols].bitcast(FP8X4),
-                scales=w_scales[:, g, cols],
-                in_=w_grouped[:].rearrange("p e n t -> p (e n t)"),
+                scales=scale_tiles()["w"][:, g, cols],
+                in_=w_grouped[(g, h)][:].rearrange("p e n t -> p (e n t)"),
             )
 
-        half = SLOTS // 2
-        g0 = [gpool.tile([P, PACK, half], F32, name="g4") for h in range(2)]
-        for t in range(PACK):
-            for h in range(2):
-                gather(0, t, g0[h], h * half, half)
-            if t == 1:
-                quantize_w(0, 0)
-            if t == 2:
-                quantize_w(0, 1)
-        for h in range(2):
-            for s in range(half // SUB):
-                quantize_slots(0, g0[h], s * SUB, h * half + s * SUB)
+        def multiply(s):
+            bank = psum.tile([P, SUB], F32, name="acc%d" % s)
+            for j in range(SUB // C):
+                e = s * SUB // C + j
+                for g in range(PASSES):
+                    nc.tensor.matmul_mx(
+                        out=bank[:, j * C:(j + 1) * C],
+                        lhsT=w_codes[:, g, e * N:(e + 1) * N].bitcast(FP8X4),
+                        lhsT_scale=scale_tiles()["w"][:, g, e * N:(e + 1) * N],
+                        rhs=x_codes[:, g, e * C:(e + 1) * C].bitcast(FP8X4),
+                        rhs_scale=scale_tiles()["x"][:, g, e * C:(e + 1) * C],
+                        start=(g == 0),
+                        stop=(g == PASSES - 1),
+                    )
+            acc[s] = bank
 
-        sums = []
-        first = 0
-        for ci, count in enumerate((1024, 512, 512)):
-            g1 = gpool.tile([P, PACK, count], F32, name="g4")
-            for t in range(PACK):
-                gather(1, t, g1, first, count)
-            if ci < 2:
-                quantize_w(1, ci)
-            for s in range(count // SUB):
-                lo = first + s * SUB
-                quantize_slots(1, g1, s * SUB, lo)
-                acc = psum.tile([P, SUB], F32, name="acc%d" % (lo // SUB))
-                for j in range(SUB // C):
-                    e = lo // C + j
-                    for g in range(PASSES):
-                        nc.tensor.matmul_mx(
-                            out=acc[:, j * C:(j + 1) * C],
-                            lhsT=w_codes[:, g, e * N:(e + 1) * N].bitcast(FP8X4),
-                            lhsT_scale=w_scales[:, g, e * N:(e + 1) * N],
-                            rhs=x_codes[:, g, e * C:(e + 1) * C].bitcast(FP8X4),
-                            rhs_scale=x_scales[:, g, e * C:(e + 1) * C],
-                            start=(g == 0),
-                            stop=(g == PASSES - 1),
-                        )
-                y = keep.tile([P, SUB], F32, name="y%d" % (lo // SUB))
-                nc.scalar.copy(out=y[:], in_=acc[:])
-                sums.append((lo, y))
-            first += count
+        def copy_sums(s):
+            y = keep.tile([P, SUB], F32, name="y%d" % s)
+            nc.scalar.copy(out=y[:], in_=acc[s][:])
+            sums[s] = y
 
-        for lo, y in sums:
+        def scatter(s):
             nc.vector.tensor_tensor(
-                window[:].indirect(offsets[:, lo // 16:(lo + SUB) // 16]),
-                y[:],
-                gate_sb[:, lo:lo + SUB],
+                window[:].indirect(offsets[:, s * SUB // 16:(s + 1) * SUB // 16]),
+                sums[s][:],
+                gate_sb[:, s * SUB:(s + 1) * SUB],
                 MULT,
             )
+
+        nc.scalar.copy(out=xb[:, 0, :], in_=planes[(0, 3)][:])
+        gather_s(0, 0)
+        gather_s(0, 1)
+        gather_s(0, 2)
+        gather_s(0, 3)
+        gather_v(0, 0, 0)
+        gather_v(0, 0, 1)
+        gather_v(0, 1, 0)
+        gather_v(0, 1, 1)
+        gather_v(0, 2, 0)
+        gather_v(0, 2, 1)
+        gather_v(1, 0, 0)
+        gather_v(1, 0, 1)
+        gather_v(1, 0, 2)
+        gather_v(1, 1, 0)
+        gather_v(1, 1, 1)
+        gather_v(1, 1, 2)
+        gather_v(1, 2, 0)
+        gather_v(1, 2, 1)
+        gather_v(1, 2, 2)
+        nc.scalar.copy(out=xb[:, 1, :], in_=planes[(1, 3)][:])
+        gather_s(1, 0)
+        gather_s(1, 1)
+        interleave_w(0, 0, "S")
+        interleave_w(1, 0, "S")
+        interleave(0, 0)
+        interleave(0, 1)
+        interleave(0, 2)
+        interleave(0, 3)
+        quantize_w(0, 0)
+        quantize_slots(0, 0)
+        quantize_slots(0, 1)
+        quantize_w(1, 0)
+        quantize_slots(0, 2)
+        quantize_slots(0, 3)
+        interleave(1, 0)
+        quantize_slots(1, 0)
+        multiply(0)
+        interleave(1, 1)
+        quantize_slots(1, 1)
+        multiply(1)
+        interleave_w(0, 1, "S")
+        quantize_w(0, 1)
+        copy_sums(0)
+        interleave_w(1, 1, "S")
+        quantize_w(1, 1)
+        copy_sums(1)
+        gather_s(1, 2)
+        interleave(1, 2)
+        quantize_slots(1, 2)
+        multiply(2)
+        gather_s(1, 3)
+        interleave(1, 3)
+        quantize_slots(1, 3)
+        multiply(3)
+        copy_sums(2)
+        copy_sums(3)
+        scatter(0)
+        scatter(1)
+        scatter(2)
+        scatter(3)
         nc.sync.dma_start(out=out, in_=window[:])

@@ -18,10 +18,11 @@ P = 128
 PACK = 4
 PASSES = K // (P * PACK)
 SLOTS = E * C
-SUB = 512
+HALF = SLOTS // 2
+BANK = 512
 W_EXPERTS = 4
 VPLANES = 3
-CHUNKS = (((0, 1024), (1024, 1024)), ((0, 1024), (1024, 512), (1536, 512)))
+RUN = 4
 
 
 def tile_routed_moe_kernel(tc, xT, w, gate, offs, out):
@@ -42,10 +43,6 @@ def tile_routed_moe_kernel(tc, xT, w, gate, offs, out):
 
         planes = {}
         w_raw = {}
-        w_grouped = {}
-        grouped = {}
-        gathered = {}
-        scales = {}
         acc = {}
         sums = {}
         gate_sb = keep.tile([P, SLOTS], F32, name="gate_sb")
@@ -78,172 +75,121 @@ def tile_routed_moe_kernel(tc, xT, w, gate, offs, out):
         nc.sync.dma_start(out=gate_sb[:], in_=gate)
 
         x_codes = keep.tile([P, PASSES, SLOTS], U32, name="x_codes", align_bytes=64)
-        w_codes = keep.tile([P, PASSES, E * N], U32, name="w_codes", align_bytes=64)
+        w_codes = keep.tile([P, 2, PASSES, W_EXPERTS * N], U32, name="w_codes", align_bytes=64)
         window = keep.tile([P, T], F32, name="window")
         xb = keep.tile([P, PASSES, T], BF16, name="xb")
 
-        def scale_tiles():
-            if not scales:
-                scales["x"] = late_p.tile([P, PASSES, SLOTS], U8, name="x_scales", offset=0, align_bytes=64)
-                scales["w"] = late_p.tile([P, PASSES, E * N], U8, name="w_scales", offset=PASSES * SLOTS, align_bytes=64)
-            return scales
+        def slots(first, count):
+            return offsets[:, first // 16:(first + count) // 16]
 
-        def gathered_tile(g, i):
-            if (g, i) not in gathered:
-                shape = [P, VPLANES, CHUNKS[g][i][1]]
-                if (g, i) == (1, 0):
-                    gathered[(g, i)] = late_a.tile(shape, F32, name="gathered1_0", offset=0)
-                else:
-                    gathered[(g, i)] = keep.tile(shape, F32, name="gathered%d_%d" % (g, i))
-            return gathered[(g, i)]
+        def gather_v(g, t, dst, first):
+            nc.vector.tensor_copy(dst[:, t, :], planes[(g, t)][:].indirect(slots(first, HALF)))
 
-        def grouped_tile(g, s):
-            if (g, s) not in grouped:
-                shape = [P, SUB, PACK]
-                if (g, s) == (1, 2):
-                    grouped[(g, s)] = late_a.tile(shape, BF16, name="grouped1_2", offset=8192, align_bytes=64)
-                elif (g, s) in ((1, 0), (1, 3)):
-                    grouped[(g, s)] = late_g.tile(shape, BF16, name="grouped1_%d" % s, offset=0, align_bytes=64)
-                else:
-                    grouped[(g, s)] = keep.tile(shape, BF16, name="grouped%d_%d" % (g, s), align_bytes=64)
-            return grouped[(g, s)]
+        def gather_s(g, dst, first, count):
+            nc.scalar.activation(out=dst[:, :, VPLANES], in_=xb[:, g, :].indirect(slots(first, count)), func=COPY)
 
-        def gather_v(g, t, i):
-            first, count = CHUNKS[g][i]
-            nc.vector.tensor_copy(gathered_tile(g, i)[:, t, :], planes[(g, t)][:].indirect(offsets[:, first // 16:(first + count) // 16]))
-
-        def gather_s(g, s):
-            nc.scalar.activation(
-                out=grouped_tile(g, s)[:, :, VPLANES],
-                in_=xb[:, g, :].indirect(offsets[:, s * SUB // 16:(s + 1) * SUB // 16]),
-                func=COPY,
+        def interleave(dst, lo, src, src_lo, count):
+            nc.scalar.copy(
+                out=dst[:, lo:lo + count, 0:VPLANES].rearrange("p (c i) t -> p c t i", i=RUN),
+                in_=src[:, :, src_lo:src_lo + count].rearrange("p t (c i) -> p c t i", i=RUN),
             )
 
-        def interleave(g, s):
-            i = [j for j, (first, count) in enumerate(CHUNKS[g]) if first <= s * SUB < first + count][0]
-            src = gathered_tile(g, i)
-            lo = s * SUB - CHUNKS[g][i][0]
-            nc.scalar.copy(out=grouped_tile(g, s)[:, :, 0:VPLANES], in_=src[:, :, lo:lo + SUB].rearrange("p t n -> p n t"))
-
-        def quantize_slots(g, s):
+        def quantize_slots(g, src, lo, first, count):
             nc.vector.quantize_mx(
-                out=x_codes[:, g, s * SUB:(s + 1) * SUB].bitcast(FP8X4),
-                scales=scale_tiles()["x"][:, g, s * SUB:(s + 1) * SUB],
-                in_=grouped_tile(g, s)[:].rearrange("p n t -> p (n t)"),
+                out=x_codes[:, g, first:first + count].bitcast(FP8X4),
+                scales=x_scales[:, g, first:first + count],
+                in_=src[:, lo:lo + count, :].rearrange("p n t -> p (n t)"),
             )
 
-        def interleave_w(g, h, engine):
-            shape = [P, W_EXPERTS, N, PACK]
-            if h == 1:
-                wg = late_a.tile(shape, BF16, name="w_grouped%d1" % g, offset=4096 * g, align_bytes=64)
-            else:
-                wg = keep.tile(shape, BF16, name="w_grouped%d0" % g, align_bytes=64)
+        def interleave_w(g, h, dst, engine):
             src = w_raw[(g, h)][:].rearrange("p e (t n) -> p e n t", t=PACK)
             if engine == "V":
-                nc.vector.tensor_copy(out=wg[:], in_=src)
+                nc.vector.tensor_copy(out=dst[:, g], in_=src)
             elif engine == "G":
-                for e in range(W_EXPERTS):
-                    nc.gpsimd.tensor_copy(out=wg[:, e], in_=src[:, e])
+                step = W_EXPERTS // 4
+                for e in range(0, W_EXPERTS, step):
+                    nc.gpsimd.tensor_copy(out=dst[:, g, e:e + step], in_=src[:, e:e + step])
             else:
-                nc.scalar.copy(out=wg[:], in_=src)
-            w_grouped[(g, h)] = wg
+                nc.scalar.copy(out=dst[:, g], in_=src)
 
-        def quantize_w(g, h):
-            cols = slice(h * W_EXPERTS * N, (h + 1) * W_EXPERTS * N)
+        def quantize_w(h, src):
             nc.vector.quantize_mx(
-                out=w_codes[:, g, cols].bitcast(FP8X4),
-                scales=scale_tiles()["w"][:, g, cols],
-                in_=w_grouped[(g, h)][:].rearrange("p e n t -> p (e n t)"),
+                out=w_codes[:, h].rearrange("p g c -> p (g c)").bitcast(FP8X4),
+                scales=w_scales[:, h].rearrange("p g c -> p (g c)"),
+                in_=src[:].rearrange("p g e n t -> p (g e n t)"),
             )
 
-        def multiply(s):
-            bank = psum.tile([P, SUB], F32, name="acc%d" % s)
-            for j in range(SUB // C):
-                e = s * SUB // C + j
+        def multiply(b):
+            bank = psum.tile([P, BANK], F32, name="acc%d" % b)
+            for j in range(BANK // C):
+                e = b * BANK // C + j
+                h, k = e // W_EXPERTS, e % W_EXPERTS
                 for g in range(PASSES):
                     nc.tensor.matmul_mx(
                         out=bank[:, j * C:(j + 1) * C],
-                        lhsT=w_codes[:, g, e * N:(e + 1) * N].bitcast(FP8X4),
-                        lhsT_scale=scale_tiles()["w"][:, g, e * N:(e + 1) * N],
+                        lhsT=w_codes[:, h, g, k * N:(k + 1) * N].bitcast(FP8X4),
+                        lhsT_scale=w_scales[:, h, g, k * N:(k + 1) * N],
                         rhs=x_codes[:, g, e * C:(e + 1) * C].bitcast(FP8X4),
-                        rhs_scale=scale_tiles()["x"][:, g, e * C:(e + 1) * C],
+                        rhs_scale=x_scales[:, g, e * C:(e + 1) * C],
                         start=(g == 0),
                         stop=(g == PASSES - 1),
                     )
-            acc[s] = bank
+            acc[b] = bank
 
-        def copy_sums(s):
-            y = keep.tile([P, SUB], F32, name="y%d" % s)
-            nc.scalar.copy(out=y[:], in_=acc[s][:])
-            sums[s] = y
+        def copy_sums(b):
+            y = keep.tile([P, BANK], F32, name="y%d" % b)
+            nc.scalar.copy(out=y[:], in_=acc[b][:])
+            sums[b] = y
 
-        def scatter(s):
-            nc.vector.tensor_tensor(
-                window[:].indirect(offsets[:, s * SUB // 16:(s + 1) * SUB // 16]),
-                sums[s][:],
-                gate_sb[:, s * SUB:(s + 1) * SUB],
-                MULT,
-            )
+        def scatter(b):
+            nc.vector.tensor_tensor(window[:].indirect(slots(b * BANK, BANK)), sums[b][:], gate_sb[:, b * BANK:(b + 1) * BANK], MULT)
 
-        nc.scalar.copy(out=xb[:, 0, :], in_=planes[(0, 3)][:])
-        gather_s(0, 0)
-        gather_s(0, 1)
-        gather_s(0, 2)
-        gather_s(0, 3)
-        gather_v(0, 0, 0)
-        gather_v(0, 0, 1)
-        gather_v(0, 1, 0)
-        gather_v(0, 1, 1)
-        gather_v(0, 2, 0)
-        gather_v(0, 2, 1)
-        gather_v(1, 0, 0)
-        gather_v(1, 0, 1)
-        gather_v(1, 0, 2)
-        gather_v(1, 1, 0)
-        gather_v(1, 1, 1)
-        gather_v(1, 1, 2)
-        gather_v(1, 2, 0)
-        gather_v(1, 2, 1)
-        gather_v(1, 2, 2)
-        nc.scalar.copy(out=xb[:, 1, :], in_=planes[(1, 3)][:])
-        gather_s(1, 0)
-        gather_s(1, 1)
-        interleave_w(0, 0, "S")
-        interleave_w(1, 0, "S")
-        interleave(0, 0)
-        interleave(0, 1)
-        interleave(0, 2)
-        interleave(0, 3)
-        quantize_w(0, 0)
-        quantize_slots(0, 0)
-        quantize_slots(0, 1)
-        quantize_w(1, 0)
-        quantize_slots(0, 2)
-        quantize_slots(0, 3)
-        interleave(1, 0)
-        quantize_slots(1, 0)
-        multiply(0)
-        interleave(1, 1)
-        quantize_slots(1, 1)
-        multiply(1)
-        interleave_w(0, 1, "S")
-        quantize_w(0, 1)
+        grouped0 = [keep.tile([P, HALF, PACK], BF16, name="grouped0_%d" % h, align_bytes=64) for h in range(2)]
+        gathered0 = [keep.tile([P, VPLANES, HALF], F32, name="gathered0_%d" % h) for h in range(2)]
+        gathered1 = [late_a.tile([P, VPLANES, HALF], F32, name="gathered1_0", offset=0), keep.tile([P, VPLANES, HALF], F32, name="gathered1_1")]
+        grouped1a = late_g.tile([P, HALF, PACK], BF16, name="grouped1a", offset=0, align_bytes=64)
+        w_grouped0 = keep.tile([P, PASSES, W_EXPERTS, N, PACK], BF16, name="w_grouped0", align_bytes=64)
+
+        nc.scalar.copy(out=xb[:, 0, :], in_=planes[(0, VPLANES)][:])
+        for h in range(2):
+            gather_s(0, grouped0[h], h * HALF, HALF)
+        for t in range(VPLANES):
+            for h in range(2):
+                gather_v(0, t, gathered0[h], h * HALF)
+        for t in range(VPLANES):
+            for h in range(2):
+                gather_v(1, t, gathered1[h], h * HALF)
+        x_scales = late_p.tile([P, PASSES, SLOTS], U8, name="x_scales", offset=0, align_bytes=64)
+        w_scales = late_p.tile([P, 2, PASSES, W_EXPERTS * N], U8, name="w_scales", offset=PASSES * SLOTS, align_bytes=64)
+
+        nc.vector.tensor_copy(out=xb[:, 1, :], in_=planes[(1, VPLANES)][:])
+        gather_s(1, grouped1a, 0, HALF)
+        interleave_w(0, 0, w_grouped0, "S")
+        interleave_w(1, 0, w_grouped0, "S")
+        for h in range(2):
+            interleave(grouped0[h], 0, gathered0[h], 0, HALF)
+        quantize_w(0, w_grouped0)
+        for h in range(2):
+            quantize_slots(0, grouped0[h], 0, h * HALF, HALF)
+        for b in range(2):
+            interleave(grouped1a, b * BANK, gathered1[0], b * BANK, BANK)
+            quantize_slots(1, grouped1a, b * BANK, b * BANK, BANK)
+            multiply(b)
+        w_grouped1 = late_a.tile([P, PASSES, W_EXPERTS, N, PACK], BF16, name="w_grouped1", offset=0, align_bytes=64)
+        interleave_w(0, 1, w_grouped1, "S")
         copy_sums(0)
-        interleave_w(1, 1, "S")
-        quantize_w(1, 1)
+        interleave_w(1, 1, w_grouped1, "V")
+        quantize_w(1, w_grouped1)
         copy_sums(1)
-        gather_s(1, 2)
-        interleave(1, 2)
-        quantize_slots(1, 2)
-        multiply(2)
-        gather_s(1, 3)
-        interleave(1, 3)
-        quantize_slots(1, 3)
-        multiply(3)
+        grouped1b = late_a.tile([P, BANK, PACK], BF16, name="grouped1b", offset=8192, align_bytes=64)
+        grouped1c = late_g.tile([P, BANK, PACK], BF16, name="grouped1c", offset=0, align_bytes=64)
+        for b, dst in ((2, grouped1b), (3, grouped1c)):
+            gather_s(1, dst, b * BANK, BANK)
+            interleave(dst, 0, gathered1[1], b * BANK - HALF, BANK)
+            quantize_slots(1, dst, 0, b * BANK, BANK)
+            multiply(b)
         copy_sums(2)
         copy_sums(3)
-        scatter(0)
-        scatter(1)
-        scatter(2)
-        scatter(3)
+        for b in range(4):
+            scatter(b)
         nc.sync.dma_start(out=out, in_=window[:])

@@ -63,9 +63,9 @@ def tile_routed_moe_kernel(tc, xT, w, gate, offs, out):
         load_plane(0, 0)
         load_plane(0, 3)
         load_plane(0, 1)
-        load_plane(1, 3)
-        load_plane(0, 2)
         load_w(0, 0)
+        load_plane(0, 2)
+        load_plane(1, 3)
         load_plane(1, 0)
         load_w(1, 0)
         load_plane(1, 1)
@@ -162,12 +162,14 @@ def tile_routed_moe_kernel(tc, xT, w, gate, offs, out):
         x_scales = late_p.tile([P, PASSES, SLOTS], U8, name="x_scales", offset=0, align_bytes=64)
         w_scales = late_p.tile([P, 2, PASSES, W_EXPERTS * N], U8, name="w_scales", offset=PASSES * SLOTS, align_bytes=64)
 
-        nc.vector.tensor_copy(out=xb[:, 1, :], in_=planes[(1, VPLANES)][:])
+        nc.scalar.copy(out=xb[:, 1, :], in_=planes[(1, VPLANES)][:])
         gather_s(1, grouped1a, 0, HALF)
-        interleave_w(0, 0, w_grouped0, "S")
-        interleave_w(1, 0, w_grouped0, "S")
+        interleave_w(0, 0, w_grouped0, "G")
+        interleave_w(1, 0, w_grouped0, "G")
         for h in range(2):
             interleave(grouped0[h], 0, gathered0[h], 0, HALF)
+        grouped1b = keep.tile([P, BANK, PACK], BF16, name="grouped1b", align_bytes=64)
+        gather_s(1, grouped1b, 2 * BANK, BANK)
         quantize_w(0, w_grouped0)
         for h in range(2):
             quantize_slots(0, grouped0[h], 0, h * HALF, HALF)
@@ -181,10 +183,10 @@ def tile_routed_moe_kernel(tc, xT, w, gate, offs, out):
         interleave_w(1, 1, w_grouped1, "V")
         quantize_w(1, w_grouped1)
         copy_sums(1)
-        grouped1b = late_a.tile([P, BANK, PACK], BF16, name="grouped1b", offset=8192, align_bytes=64)
         grouped1c = late_g.tile([P, BANK, PACK], BF16, name="grouped1c", offset=0, align_bytes=64)
         for b, dst in ((2, grouped1b), (3, grouped1c)):
-            gather_s(1, dst, b * BANK, BANK)
+            if b == 3:
+                gather_s(1, dst, b * BANK, BANK)
             interleave(dst, 0, gathered1[1], b * BANK - HALF, BANK)
             quantize_slots(1, dst, 0, b * BANK, BANK)
             multiply(b)

@@ -69,9 +69,9 @@ def tile_routed_moe_kernel(tc, xT, w, gate, offs, out):
         load_plane(1, 0)
         load_w(1, 0)
         load_plane(1, 1)
+        load_plane(1, 2)
         load_w(0, 1)
         load_w(1, 1)
-        load_plane(1, 2)
         nc.sync.dma_start(out=gate_sb[:], in_=gate)
 
         x_codes = keep.tile([P, PASSES, SLOTS], U32, name="x_codes", align_bytes=64)

@@ -21,8 +21,6 @@ SLOTS = E * C
 HALF = SLOTS // 2
 BANK = 512
 W_EXPERTS = 4
-VPLANES = 3
-RUN = 4
 
 
 def tile_routed_moe_kernel(tc, xT, w, gate, offs, out):
@@ -34,8 +32,6 @@ def tile_routed_moe_kernel(tc, xT, w, gate, offs, out):
         keep = ctx.enter_context(tc.tile_pool(name="keep", bufs=1))
         stage = ctx.enter_context(tc.tile_pool(name="stage", bufs=8))
         late_p = ctx.enter_context(tc.tile_pool(name="late_p", bufs=1))
-        late_a = ctx.enter_context(tc.tile_pool(name="late_a", bufs=1))
-        late_g = ctx.enter_context(tc.tile_pool(name="late_g", bufs=1))
         psum = ctx.enter_context(tc.psum_pool(name="psum", bufs=1))
 
         offsets = keep.tile([P, SLOTS // 16], U16, name="offsets")
@@ -48,8 +44,8 @@ def tile_routed_moe_kernel(tc, xT, w, gate, offs, out):
         gate_sb = keep.tile([P, SLOTS], F32, name="gate_sb")
 
         def load_plane(g, t):
-            if (g, t) == (1, VPLANES - 1):
-                raw = late_p.tile([P, T], F32, name="last_plane", offset=0)
+            if g == 1 and t < 2:
+                raw = late_p.tile([P, T], F32, name="late_plane%d" % t, offset=t * T * 4)
             else:
                 raw = stage.tile([P, T], F32, name="raw")
             nc.sync.dma_start(out=raw[:], in_=x_planes[g, :, t, :])
@@ -61,62 +57,88 @@ def tile_routed_moe_kernel(tc, xT, w, gate, offs, out):
             w_raw[(g, h)] = raw
 
         load_plane(0, 0)
-        load_plane(0, 3)
+        load_plane(0, 2)
         load_plane(0, 1)
         load_w(0, 0)
-        load_plane(0, 2)
-        load_plane(1, 3)
         load_plane(1, 0)
-        load_w(1, 0)
+        load_plane(0, 3)
         load_plane(1, 1)
+        load_w(1, 0)
         load_plane(1, 2)
+        load_plane(1, 3)
         load_w(0, 1)
         load_w(1, 1)
         nc.sync.dma_start(out=gate_sb[:], in_=gate)
 
         x_codes = keep.tile([P, PASSES, SLOTS], U32, name="x_codes", align_bytes=64)
+        x_scales = keep.tile([P, PASSES, SLOTS], U8, name="x_scales", align_bytes=64)
         w_codes = keep.tile([P, 2, PASSES, W_EXPERTS * N], U32, name="w_codes", align_bytes=64)
+        w_scales = keep.tile([P, 2, PASSES, W_EXPERTS * N], U8, name="w_scales", align_bytes=64)
         window = keep.tile([P, T], F32, name="window")
-        xb = keep.tile([P, PASSES, T], BF16, name="xb")
+        xb = keep.tile([P, PASSES, 2, T], BF16, name="xb")
+
+        span = (SLOTS, HALF)
+        pairs = {}
+        grouped = {}
+        for g in range(PASSES):
+            for c in range(SLOTS // span[g]):
+                pairs[(g, c)] = keep.tile([P, 2, span[g], 2], BF16, name="pairs%d_%d" % (g, c), align_bytes=64)
+        w_grouped = [keep.tile([P, PASSES, W_EXPERTS, N, PACK], BF16, name="w_grouped%d" % h, align_bytes=64) for h in range(2)]
 
         def slots(first, count):
             return offsets[:, first // 16:(first + count) // 16]
 
-        def gather_v(g, t, dst, first):
-            nc.vector.tensor_copy(dst[:, t, :], planes[(g, t)][:].indirect(slots(first, HALF)))
+        def cast(g, t):
+            nc.scalar.copy(out=xb[:, g, t - 2, :], in_=planes[(g, t)][:])
 
-        def gather_s(g, dst, first, count):
-            nc.scalar.activation(out=dst[:, :, VPLANES], in_=xb[:, g, :].indirect(slots(first, count)), func=COPY)
+        def pair_slice(g, first, count):
+            lo = first % span[g]
+            return pairs[(g, first // span[g])][:, :, lo:lo + count, :]
 
-        def interleave(dst, lo, src, src_lo, count):
-            nc.scalar.copy(
-                out=dst[:, lo:lo + count, 0:VPLANES].rearrange("p (c i) t -> p c t i", i=RUN),
-                in_=src[:, :, src_lo:src_lo + count].rearrange("p t (c i) -> p c t i", i=RUN),
+        def gather_v(g, t, first, count):
+            nc.vector.tensor_copy(pair_slice(g, first, count)[:, 0, :, t], planes[(g, t)][:].indirect(slots(first, count)))
+
+        def gather_s(g, t, first, count):
+            nc.scalar.activation(out=pair_slice(g, first, count)[:, 1, :, t - 2], in_=xb[:, g, t - 2, :].indirect(slots(first, count)), func=COPY)
+
+        def interleave(g, first, count):
+            if g == 0:
+                whole = late_p.tile([P, count, PACK], BF16, name="grouped0", offset=0, align_bytes=64)
+            else:
+                whole = keep.tile([P, count, PACK], BF16, name="grouped1_%d" % first, align_bytes=64)
+            grouped[g] = (whole, first)
+            tile_of = pairs[(g, first // span[g])]
+            lo = first % span[g]
+            words = tile_of[:].rearrange("p u s e -> p (u s e)").bitcast(F32).rearrange("p (u s) -> p u s", u=2)
+            nc.vector.tensor_copy(
+                out=whole[:].rearrange("p s t -> p (s t)").bitcast(F32).rearrange("p (s u) -> p s u", u=2),
+                in_=words[:, :, lo:lo + count].rearrange("p u s -> p s u"),
             )
 
-        def quantize_slots(g, src, lo, first, count):
+        def quantize_slots(g, first, count):
+            whole, base = grouped[g]
             nc.vector.quantize_mx(
                 out=x_codes[:, g, first:first + count].bitcast(FP8X4),
                 scales=x_scales[:, g, first:first + count],
-                in_=src[:, lo:lo + count, :].rearrange("p n t -> p (n t)"),
+                in_=whole[:, first - base:first - base + count, :].rearrange("p s t -> p (s t)"),
             )
 
-        def interleave_w(g, h, dst, engine):
+        def interleave_w(g, h, engine):
             src = w_raw[(g, h)][:].rearrange("p e (t n) -> p e n t", t=PACK)
+            dst = w_grouped[h]
             if engine == "V":
                 nc.vector.tensor_copy(out=dst[:, g], in_=src)
             elif engine == "G":
-                step = W_EXPERTS // 4
-                for e in range(0, W_EXPERTS, step):
-                    nc.gpsimd.tensor_copy(out=dst[:, g, e:e + step], in_=src[:, e:e + step])
+                for e in range(W_EXPERTS):
+                    nc.gpsimd.tensor_copy(out=dst[:, g, e:e + 1], in_=src[:, e:e + 1])
             else:
                 nc.scalar.copy(out=dst[:, g], in_=src)
 
-        def quantize_w(h, src):
+        def quantize_w(h):
             nc.vector.quantize_mx(
                 out=w_codes[:, h].rearrange("p g c -> p (g c)").bitcast(FP8X4),
                 scales=w_scales[:, h].rearrange("p g c -> p (g c)"),
-                in_=src[:].rearrange("p g e n t -> p (g e n t)"),
+                in_=w_grouped[h][:].rearrange("p g e n t -> p (g e n t)"),
             )
 
         def multiply(b):
@@ -138,60 +160,60 @@ def tile_routed_moe_kernel(tc, xT, w, gate, offs, out):
 
         def copy_sums(b):
             y = keep.tile([P, BANK], F32, name="y%d" % b)
-            nc.scalar.copy(out=y[:], in_=acc[b][:])
+            if b == 0:
+                nc.vector.tensor_copy(out=y[:], in_=acc[b][:])
+            else:
+                nc.scalar.copy(out=y[:], in_=acc[b][:])
             sums[b] = y
 
         def scatter(b):
             nc.vector.tensor_tensor(window[:].indirect(slots(b * BANK, BANK)), sums[b][:], gate_sb[:, b * BANK:(b + 1) * BANK], MULT)
 
-        grouped0 = [keep.tile([P, HALF, PACK], BF16, name="grouped0_%d" % h, align_bytes=64) for h in range(2)]
-        gathered0 = [keep.tile([P, VPLANES, HALF], F32, name="gathered0_%d" % h) for h in range(2)]
-        gathered1 = [late_a.tile([P, VPLANES, HALF], F32, name="gathered1_0", offset=0), keep.tile([P, VPLANES, HALF], F32, name="gathered1_1")]
-        grouped1a = late_g.tile([P, HALF, PACK], BF16, name="grouped1a", offset=0, align_bytes=64)
-        w_grouped0 = keep.tile([P, PASSES, W_EXPERTS, N, PACK], BF16, name="w_grouped0", align_bytes=64)
-
-        nc.scalar.copy(out=xb[:, 0, :], in_=planes[(0, VPLANES)][:])
-        for h in range(2):
-            gather_s(0, grouped0[h], h * HALF, HALF)
-        for t in range(VPLANES):
+        cast(0, 2)
+        for t in range(2):
             for h in range(2):
-                gather_v(0, t, gathered0[h], h * HALF)
-        for t in range(VPLANES):
+                gather_v(0, t, h * HALF, HALF)
+        for h in range(2):
+            gather_s(0, 2, h * HALF, HALF)
+        cast(0, 3)
+        for h in range(2):
+            gather_s(0, 3, h * HALF, HALF)
+        interleave_w(0, 0, "G")
+        for t in range(2):
             for h in range(2):
-                gather_v(1, t, gathered1[h], h * HALF)
-        x_scales = late_p.tile([P, PASSES, SLOTS], U8, name="x_scales", offset=0, align_bytes=64)
-        w_scales = late_p.tile([P, 2, PASSES, W_EXPERTS * N], U8, name="w_scales", offset=PASSES * SLOTS, align_bytes=64)
-
-        nc.scalar.copy(out=xb[:, 1, :], in_=planes[(1, VPLANES)][:])
-        gather_s(1, grouped1a, 0, HALF)
-        interleave_w(0, 0, w_grouped0, "G")
-        interleave_w(1, 0, w_grouped0, "G")
+                gather_v(1, t, h * HALF, HALF)
+        cast(1, 2)
+        cast(1, 3)
+        interleave(0, 0, SLOTS)
+        interleave_w(1, 0, "V")
         for h in range(2):
-            interleave(grouped0[h], 0, gathered0[h], 0, HALF)
-        grouped1b = keep.tile([P, BANK, PACK], BF16, name="grouped1b", align_bytes=64)
-        gather_s(1, grouped1b, 2 * BANK, BANK)
-        quantize_w(0, w_grouped0)
-        for h in range(2):
-            quantize_slots(0, grouped0[h], 0, h * HALF, HALF)
+            quantize_slots(0, h * HALF, HALF)
+        quantize_w(0)
         for b in range(2):
-            interleave(grouped1a, b * BANK, gathered1[0], b * BANK, BANK)
-            quantize_slots(1, grouped1a, b * BANK, b * BANK, BANK)
+            gather_s(1, 2, b * BANK, BANK)
+            gather_s(1, 3, b * BANK, BANK)
+            interleave(1, b * BANK, BANK)
+            quantize_slots(1, b * BANK, BANK)
             multiply(b)
-        w_grouped1 = late_a.tile([P, PASSES, W_EXPERTS, N, PACK], BF16, name="w_grouped1", offset=0, align_bytes=64)
-        interleave_w(0, 1, w_grouped1, "S")
+        gather_s(1, 2, 2 * BANK, BANK)
+        gather_s(1, 3, 2 * BANK, BANK)
         copy_sums(0)
-        interleave_w(1, 1, w_grouped1, "V")
-        quantize_w(1, w_grouped1)
         copy_sums(1)
-        grouped1c = late_g.tile([P, BANK, PACK], BF16, name="grouped1c", offset=0, align_bytes=64)
-        for b, dst in ((2, grouped1b), (3, grouped1c)):
-            if b == 3:
-                gather_s(1, dst, b * BANK, BANK)
-            interleave(dst, 0, gathered1[1], b * BANK - HALF, BANK)
-            quantize_slots(1, dst, 0, b * BANK, BANK)
-            multiply(b)
+        scatter(0)
+        interleave_w(0, 1, "S")
+        interleave_w(1, 1, "S")
+        interleave(1, 2 * BANK, BANK)
+        quantize_slots(1, 2 * BANK, BANK)
+        gather_s(1, 2, 3 * BANK, BANK)
+        gather_s(1, 3, 3 * BANK, BANK)
+        scatter(1)
+        quantize_w(1)
+        multiply(2)
         copy_sums(2)
+        interleave(1, 3 * BANK, BANK)
+        quantize_slots(1, 3 * BANK, BANK)
+        multiply(3)
         copy_sums(3)
-        for b in range(4):
-            scatter(b)
+        scatter(2)
+        scatter(3)
         nc.sync.dma_start(out=out, in_=window[:])

@@ -20,13 +20,15 @@ PASSES = K // (P * PACK)
 SLOTS = E * C
 HALF = SLOTS // 2
 BANK = 512
-W_EXPERTS = 4
+BANKS = SLOTS // BANK
+W_BLOCKS = E * PASSES // BANKS
+RUN = 4
 
 
 def tile_routed_moe_kernel(tc, xT, w, gate, offs, out):
     nc = tc.nc
     x_planes = xT.rearrange("(g p t) n -> g p t n", g=PASSES, p=P, t=PACK)
-    w_rows = w.rearrange("e (g p t) n -> g p e (t n)", g=PASSES, p=P, t=PACK)
+    w_rows = w.rearrange("e (g p t) n -> p (e g) (t n)", g=PASSES, p=P, t=PACK)
 
     with ExitStack() as ctx:
         keep = ctx.enter_context(tc.tile_pool(name="keep", bufs=1))
@@ -45,35 +47,34 @@ def tile_routed_moe_kernel(tc, xT, w, gate, offs, out):
 
         def load_plane(g, t):
             if g == 1 and t < 2:
-                raw = late_p.tile([P, T], F32, name="late_plane%d" % t, offset=t * T * 4)
+                raw = late_p.tile([P, T], F32, name="late_plane%d" % t, offset=(1 - t) * T * 4)
             else:
                 raw = stage.tile([P, T], F32, name="raw")
             nc.sync.dma_start(out=raw[:], in_=x_planes[g, :, t, :])
             planes[(g, t)] = raw
 
-        def load_w(g, h):
-            raw = stage.tile([P, W_EXPERTS, PACK * N], F32, name="raw")
-            nc.sync.dma_start(out=raw[:], in_=w_rows[g, :, h * W_EXPERTS:(h + 1) * W_EXPERTS, :])
-            w_raw[(g, h)] = raw
+        def load_w(b):
+            raw = stage.tile([P, W_BLOCKS, PACK * N], F32, name="raw")
+            nc.sync.dma_start(out=raw[:], in_=w_rows[:, b * W_BLOCKS:(b + 1) * W_BLOCKS, :])
+            w_raw[b] = raw
 
         load_plane(0, 0)
         load_plane(0, 2)
         load_plane(0, 1)
-        load_w(0, 0)
+        load_w(0)
         load_plane(1, 0)
         load_plane(0, 3)
         load_plane(1, 1)
-        load_w(1, 0)
+        load_w(1)
         load_plane(1, 2)
         load_plane(1, 3)
-        load_w(0, 1)
-        load_w(1, 1)
+        load_w(2)
+        load_w(3)
         nc.sync.dma_start(out=gate_sb[:], in_=gate)
 
         x_codes = keep.tile([P, PASSES, SLOTS], U32, name="x_codes", align_bytes=64)
         x_scales = keep.tile([P, PASSES, SLOTS], U8, name="x_scales", align_bytes=64)
-        w_codes = keep.tile([P, 2, PASSES, W_EXPERTS * N], U32, name="w_codes", align_bytes=64)
-        w_scales = keep.tile([P, 2, PASSES, W_EXPERTS * N], U8, name="w_scales", align_bytes=64)
+        w_codes = keep.tile([P, BANKS, W_BLOCKS * N], U32, name="w_codes", align_bytes=64)
         window = keep.tile([P, T], F32, name="window")
         xb = keep.tile([P, PASSES, 2, T], BF16, name="xb")
 
@@ -83,7 +84,7 @@ def tile_routed_moe_kernel(tc, xT, w, gate, offs, out):
         for g in range(PASSES):
             for c in range(SLOTS // span[g]):
                 pairs[(g, c)] = keep.tile([P, 2, span[g], 2], BF16, name="pairs%d_%d" % (g, c), align_bytes=64)
-        w_grouped = [keep.tile([P, PASSES, W_EXPERTS, N, PACK], BF16, name="w_grouped%d" % h, align_bytes=64) for h in range(2)]
+        w_grouped = [keep.tile([P, W_BLOCKS, N, PACK], BF16, name="w_grouped%d" % b, align_bytes=64) for b in range(BANKS)]
 
         def slots(first, count):
             return offsets[:, first // 16:(first + count) // 16]
@@ -103,7 +104,7 @@ def tile_routed_moe_kernel(tc, xT, w, gate, offs, out):
 
         def interleave(g, first, count):
             if g == 0:
-                whole = late_p.tile([P, count, PACK], BF16, name="grouped0", offset=0, align_bytes=64)
+                whole = late_p.tile([P, count, PACK], BF16, name="grouped0", offset=BANKS * W_BLOCKS * N, align_bytes=64)
             else:
                 whole = keep.tile([P, count, PACK], BF16, name="grouped1_%d" % first, align_bytes=64)
             grouped[g] = (whole, first)
@@ -123,34 +124,37 @@ def tile_routed_moe_kernel(tc, xT, w, gate, offs, out):
                 in_=whole[:, first - base:first - base + count, :].rearrange("p s t -> p (s t)"),
             )
 
-        def interleave_w(g, h, engine):
-            src = w_raw[(g, h)][:].rearrange("p e (t n) -> p e n t", t=PACK)
-            dst = w_grouped[h]
-            if engine == "V":
-                nc.vector.tensor_copy(out=dst[:, g], in_=src)
-            elif engine == "G":
-                for e in range(W_EXPERTS):
-                    nc.gpsimd.tensor_copy(out=dst[:, g, e:e + 1], in_=src[:, e:e + 1])
+        def interleave_w(b, engine):
+            dst = w_grouped[b]
+            if engine == "G":
+                src = w_raw[b][:].rearrange("p x (t n) -> p x n t", t=PACK)
+                for x in range(W_BLOCKS):
+                    nc.gpsimd.tensor_copy(out=dst[:, x:x + 1], in_=src[:, x:x + 1])
             else:
-                nc.scalar.copy(out=dst[:, g], in_=src)
+                runs_in = w_raw[b][:].rearrange("p x (t c i) -> p x c t i", t=PACK, i=RUN)
+                runs_out = dst[:].rearrange("p x (c i) t -> p x c t i", i=RUN)
+                if engine == "V":
+                    nc.vector.tensor_copy(out=runs_out, in_=runs_in)
+                else:
+                    nc.scalar.copy(out=runs_out, in_=runs_in)
 
-        def quantize_w(h):
+        def quantize_w(b):
             nc.vector.quantize_mx(
-                out=w_codes[:, h].rearrange("p g c -> p (g c)").bitcast(FP8X4),
-                scales=w_scales[:, h].rearrange("p g c -> p (g c)"),
-                in_=w_grouped[h][:].rearrange("p g e n t -> p (g e n t)"),
+                out=w_codes[:, b, :].bitcast(FP8X4),
+                scales=w_scales[:, b, :],
+                in_=w_grouped[b][:].rearrange("p x n t -> p (x n t)"),
             )
 
         def multiply(b):
             bank = psum.tile([P, BANK], F32, name="acc%d" % b)
             for j in range(BANK // C):
                 e = b * BANK // C + j
-                h, k = e // W_EXPERTS, e % W_EXPERTS
                 for g in range(PASSES):
+                    x = j * PASSES + g
                     nc.tensor.matmul_mx(
                         out=bank[:, j * C:(j + 1) * C],
-                        lhsT=w_codes[:, h, g, k * N:(k + 1) * N].bitcast(FP8X4),
-                        lhsT_scale=w_scales[:, h, g, k * N:(k + 1) * N],
+                        lhsT=w_codes[:, b, x * N:(x + 1) * N].bitcast(FP8X4),
+                        lhsT_scale=w_scales[:, b, x * N:(x + 1) * N],
                         rhs=x_codes[:, g, e * C:(e + 1) * C].bitcast(FP8X4),
                         rhs_scale=x_scales[:, g, e * C:(e + 1) * C],
                         start=(g == 0),
@@ -178,40 +182,47 @@ def tile_routed_moe_kernel(tc, xT, w, gate, offs, out):
         cast(0, 3)
         for h in range(2):
             gather_s(0, 3, h * HALF, HALF)
-        interleave_w(0, 0, "G")
+        interleave_w(0, "G")
         for t in range(2):
             for h in range(2):
                 gather_v(1, t, h * HALF, HALF)
+        w_scales = late_p.tile([P, BANKS, W_BLOCKS * N], U8, name="w_scales", offset=0, align_bytes=64)
         cast(1, 2)
         cast(1, 3)
         interleave(0, 0, SLOTS)
-        interleave_w(1, 0, "V")
-        for h in range(2):
-            quantize_slots(0, h * HALF, HALF)
         quantize_w(0)
-        for b in range(2):
-            gather_s(1, 2, b * BANK, BANK)
-            gather_s(1, 3, b * BANK, BANK)
-            interleave(1, b * BANK, BANK)
-            quantize_slots(1, b * BANK, BANK)
-            multiply(b)
+        quantize_slots(0, 0, HALF)
+        interleave_w(1, "V")
+        quantize_slots(0, HALF, HALF)
+        gather_s(1, 2, 0, BANK)
+        gather_s(1, 3, 0, BANK)
+        interleave(1, 0, BANK)
+        quantize_slots(1, 0, BANK)
+        multiply(0)
+        quantize_w(1)
+        gather_s(1, 2, BANK, BANK)
+        gather_s(1, 3, BANK, BANK)
+        interleave(1, BANK, BANK)
+        quantize_slots(1, BANK, BANK)
+        multiply(1)
         gather_s(1, 2, 2 * BANK, BANK)
         gather_s(1, 3, 2 * BANK, BANK)
         copy_sums(0)
         copy_sums(1)
         scatter(0)
-        interleave_w(0, 1, "S")
-        interleave_w(1, 1, "S")
+        interleave_w(2, "S")
         interleave(1, 2 * BANK, BANK)
         quantize_slots(1, 2 * BANK, BANK)
+        quantize_w(2)
+        multiply(2)
         gather_s(1, 2, 3 * BANK, BANK)
         gather_s(1, 3, 3 * BANK, BANK)
         scatter(1)
-        quantize_w(1)
-        multiply(2)
         copy_sums(2)
+        interleave_w(3, "S")
         interleave(1, 3 * BANK, BANK)
         quantize_slots(1, 3 * BANK, BANK)
+        quantize_w(3)
         multiply(3)
         copy_sums(3)
         scatter(2)

@@ -45,12 +45,14 @@ def tile_routed_moe_kernel(tc, xT, w, gate, offs, out):
         sums = {}
         gate_sb = keep.tile([P, SLOTS], F32, name="gate_sb")
 
-        def load_plane(g, t):
+        def load_plane(g, t, pieces=1):
             if g == 1 and t < 2:
                 raw = late_p.tile([P, T], F32, name="late_plane%d" % t, offset=(1 - t) * T * 4)
             else:
                 raw = stage.tile([P, T], F32, name="raw")
-            nc.sync.dma_start(out=raw[:], in_=x_planes[g, :, t, :])
+            for c in range(pieces):
+                cols = slice(c * T // pieces, (c + 1) * T // pieces)
+                nc.sync.dma_start(out=raw[:, cols], in_=x_planes[g, :, t, cols])
             planes[(g, t)] = raw
 
         def load_w(b):
@@ -59,18 +61,18 @@ def tile_routed_moe_kernel(tc, xT, w, gate, offs, out):
             w_raw[b] = raw
 
         load_plane(0, 0)
-        load_plane(0, 2)
+        load_plane(0, 2, 2)
         load_plane(0, 1)
-        load_w(0)
-        load_plane(1, 0)
         load_plane(0, 3)
+        load_plane(1, 0)
+        load_w(0)
         load_plane(1, 1)
-        load_w(1)
         load_plane(1, 2)
         load_plane(1, 3)
+        load_w(1)
+        nc.sync.dma_start(out=gate_sb[:], in_=gate)
         load_w(2)
         load_w(3)
-        nc.sync.dma_start(out=gate_sb[:], in_=gate)
 
         x_codes = keep.tile([P, PASSES, SLOTS], U32, name="x_codes", align_bytes=64)
         x_scales = keep.tile([P, PASSES, SLOTS], U8, name="x_scales", align_bytes=64)
@@ -89,8 +91,10 @@ def tile_routed_moe_kernel(tc, xT, w, gate, offs, out):
         def slots(first, count):
             return offsets[:, first // 16:(first + count) // 16]
 
-        def cast(g, t):
-            nc.scalar.copy(out=xb[:, g, t - 2, :], in_=planes[(g, t)][:])
+        def cast(g, t, pieces=1):
+            for c in range(pieces):
+                cols = slice(c * T // pieces, (c + 1) * T // pieces)
+                nc.scalar.copy(out=xb[:, g, t - 2, cols], in_=planes[(g, t)][:, cols])
 
         def pair_slice(g, first, count):
             lo = first % span[g]
@@ -124,15 +128,15 @@ def tile_routed_moe_kernel(tc, xT, w, gate, offs, out):
                 in_=whole[:, first - base:first - base + count, :].rearrange("p s t -> p (s t)"),
             )
 
-        def interleave_w(b, engine):
+        def interleave_w(b, engine, first=0, count=W_BLOCKS):
             dst = w_grouped[b]
             if engine == "G":
                 src = w_raw[b][:].rearrange("p x (t n) -> p x n t", t=PACK)
                 for x in range(W_BLOCKS):
                     nc.gpsimd.tensor_copy(out=dst[:, x:x + 1], in_=src[:, x:x + 1])
             else:
-                runs_in = w_raw[b][:].rearrange("p x (t c i) -> p x c t i", t=PACK, i=RUN)
-                runs_out = dst[:].rearrange("p x (c i) t -> p x c t i", i=RUN)
+                runs_in = w_raw[b][:, first:first + count, :].rearrange("p x (t c i) -> p x c t i", t=PACK, i=RUN)
+                runs_out = dst[:, first:first + count].rearrange("p x (c i) t -> p x c t i", i=RUN)
                 if engine == "V":
                     nc.vector.tensor_copy(out=runs_out, in_=runs_in)
                 else:
@@ -173,7 +177,7 @@ def tile_routed_moe_kernel(tc, xT, w, gate, offs, out):
         def scatter(b):
             nc.vector.tensor_tensor(window[:].indirect(slots(b * BANK, BANK)), sums[b][:], gate_sb[:, b * BANK:(b + 1) * BANK], MULT)
 
-        cast(0, 2)
+        cast(0, 2, 2)
         for t in range(2):
             for h in range(2):
                 gather_v(0, t, h * HALF, HALF)
@@ -192,17 +196,18 @@ def tile_routed_moe_kernel(tc, xT, w, gate, offs, out):
         interleave(0, 0, SLOTS)
         quantize_w(0)
         quantize_slots(0, 0, HALF)
-        interleave_w(1, "V")
-        quantize_slots(0, HALF, HALF)
+        interleave_w(1, "V", W_BLOCKS // 2, W_BLOCKS // 2)
         gather_s(1, 2, 0, BANK)
         gather_s(1, 3, 0, BANK)
+        interleave_w(1, "S", 0, W_BLOCKS // 2)
         interleave(1, 0, BANK)
+        quantize_slots(0, HALF, HALF)
         quantize_slots(1, 0, BANK)
         multiply(0)
-        quantize_w(1)
         gather_s(1, 2, BANK, BANK)
         gather_s(1, 3, BANK, BANK)
         interleave(1, BANK, BANK)
+        quantize_w(1)
         quantize_slots(1, BANK, BANK)
         multiply(1)
         gather_s(1, 2, 2 * BANK, BANK)
@@ -212,8 +217,8 @@ def tile_routed_moe_kernel(tc, xT, w, gate, offs, out):
         scatter(0)
         interleave_w(2, "S")
         interleave(1, 2 * BANK, BANK)
-        quantize_slots(1, 2 * BANK, BANK)
         quantize_w(2)
+        quantize_slots(1, 2 * BANK, BANK)
         multiply(2)
         gather_s(1, 2, 3 * BANK, BANK)
         gather_s(1, 3, 3 * BANK, BANK)
@@ -221,10 +226,11 @@ def tile_routed_moe_kernel(tc, xT, w, gate, offs, out):
         copy_sums(2)
         interleave_w(3, "S")
         interleave(1, 3 * BANK, BANK)
-        quantize_slots(1, 3 * BANK, BANK)
         quantize_w(3)
+        quantize_slots(1, 3 * BANK, BANK)
         multiply(3)
         copy_sums(3)
         scatter(2)
         scatter(3)
-        nc.sync.dma_start(out=out, in_=window[:])
+        nc.sync.dma_start(out=out[:, 0:T // 2], in_=window[:, 0:T // 2])
+        nc.scalar.dma_start(out=out[:, T // 2:T], in_=window[:, T // 2:T])

@@ -210,8 +210,8 @@ def tile_routed_moe_kernel(tc, xT, w, gate, offs, out):
         quantize_w(1)
         quantize_slots(1, BANK, BANK)
         multiply(1)
-        gather_s(1, 2, 2 * BANK, BANK)
-        gather_s(1, 3, 2 * BANK, BANK)
+        gather_s(1, 2, HALF, HALF)
+        gather_s(1, 3, HALF, HALF)
         copy_sums(0)
         copy_sums(1)
         scatter(0)
@@ -220,8 +220,6 @@ def tile_routed_moe_kernel(tc, xT, w, gate, offs, out):
         quantize_w(2)
         quantize_slots(1, 2 * BANK, BANK)
         multiply(2)
-        gather_s(1, 2, 3 * BANK, BANK)
-        gather_s(1, 3, 3 * BANK, BANK)
         scatter(1)
         copy_sums(2)
         interleave_w(3, "S")
@@ -232,5 +230,4 @@ def tile_routed_moe_kernel(tc, xT, w, gate, offs, out):
         copy_sums(3)
         scatter(2)
         scatter(3)
-        nc.sync.dma_start(out=out[:, 0:T // 2], in_=window[:, 0:T // 2])
-        nc.scalar.dma_start(out=out[:, T // 2:T], in_=window[:, T // 2:T])
+        nc.sync.dma_start(out=out, in_=window[:])

@@ -91,10 +91,13 @@ def tile_routed_moe_kernel(tc, xT, w, gate, offs, out):
         def slots(first, count):
             return offsets[:, first // 16:(first + count) // 16]
 
-        def cast(g, t, pieces=1):
+        def cast(g, t, pieces=1, engine="S"):
             for c in range(pieces):
                 cols = slice(c * T // pieces, (c + 1) * T // pieces)
-                nc.scalar.copy(out=xb[:, g, t - 2, cols], in_=planes[(g, t)][:, cols])
+                if engine == "G":
+                    nc.gpsimd.tensor_copy(out=xb[:, g, t - 2, cols], in_=planes[(g, t)][:, cols])
+                else:
+                    nc.scalar.copy(out=xb[:, g, t - 2, cols], in_=planes[(g, t)][:, cols])
 
         def pair_slice(g, first, count):
             lo = first % span[g]
@@ -183,7 +186,7 @@ def tile_routed_moe_kernel(tc, xT, w, gate, offs, out):
                 gather_v(0, t, h * HALF, HALF)
         for h in range(2):
             gather_s(0, 2, h * HALF, HALF)
-        cast(0, 3)
+        cast(0, 3, 2, "G")
         for h in range(2):
             gather_s(0, 3, h * HALF, HALF)
         interleave_w(0, "G")

@@ -75,7 +75,6 @@ def tile_routed_moe_kernel(tc, xT, w, gate, offs, out):
         load_w(3)
 
         x_codes = keep.tile([P, PASSES, SLOTS], U32, name="x_codes", align_bytes=64)
-        x_scales = keep.tile([P, PASSES, SLOTS], U8, name="x_scales", align_bytes=64)
         w_codes = keep.tile([P, BANKS, W_BLOCKS * N], U32, name="w_codes", align_bytes=64)
         window = keep.tile([P, T], F32, name="window")
         xb = keep.tile([P, PASSES, 2, T], BF16, name="xb")
@@ -109,19 +108,19 @@ def tile_routed_moe_kernel(tc, xT, w, gate, offs, out):
         def gather_s(g, t, first, count):
             nc.scalar.activation(out=pair_slice(g, first, count)[:, 1, :, t - 2], in_=xb[:, g, t - 2, :].indirect(slots(first, count)), func=COPY)
 
-        def interleave(g, first, count):
-            if g == 0:
-                whole = late_p.tile([P, count, PACK], BF16, name="grouped0", offset=BANKS * W_BLOCKS * N, align_bytes=64)
-            else:
-                whole = keep.tile([P, count, PACK], BF16, name="grouped1_%d" % first, align_bytes=64)
+        def interleave(g, first, count, pieces=1):
+            whole = keep.tile([P, count, PACK], BF16, name="grouped%d_%d" % (g, first), align_bytes=64)
             grouped[g] = (whole, first)
             tile_of = pairs[(g, first // span[g])]
             lo = first % span[g]
             words = tile_of[:].rearrange("p u s e -> p (u s e)").bitcast(F32).rearrange("p (u s) -> p u s", u=2)
-            nc.vector.tensor_copy(
-                out=whole[:].rearrange("p s t -> p (s t)").bitcast(F32).rearrange("p (s u) -> p s u", u=2),
-                in_=words[:, :, lo:lo + count].rearrange("p u s -> p s u"),
-            )
+            words_out = whole[:].rearrange("p s t -> p (s t)").bitcast(F32).rearrange("p (s u) -> p s u", u=2)
+            if g == 0:
+                step = count // pieces
+                for c in range(pieces):
+                    nc.gpsimd.tensor_copy(out=words_out[:, c * step:(c + 1) * step, :], in_=words[:, :, lo + c * step:lo + (c + 1) * step].rearrange("p u s -> p s u"))
+            else:
+                nc.vector.tensor_copy(out=words_out, in_=words[:, :, lo:lo + count].rearrange("p u s -> p s u"))
 
         def quantize_slots(g, first, count):
             whole, base = grouped[g]
@@ -194,9 +193,10 @@ def tile_routed_moe_kernel(tc, xT, w, gate, offs, out):
             for h in range(2):
                 gather_v(1, t, h * HALF, HALF)
         w_scales = late_p.tile([P, BANKS, W_BLOCKS * N], U8, name="w_scales", offset=0, align_bytes=64)
+        x_scales = late_p.tile([P, PASSES, SLOTS], U8, name="x_scales", offset=BANKS * W_BLOCKS * N, align_bytes=64)
         cast(1, 2)
         cast(1, 3)
-        interleave(0, 0, SLOTS)
+        interleave(0, 0, SLOTS, 4)
         quantize_w(0)
         quantize_slots(0, 0, HALF)
         interleave_w(1, "V", W_BLOCKS // 2, W_BLOCKS // 2)

@@ -32,8 +32,10 @@ def tile_routed_moe_kernel(tc, xT, w, gate, offs, out):
 
     with ExitStack() as ctx:
         keep = ctx.enter_context(tc.tile_pool(name="keep", bufs=1))
-        stage = ctx.enter_context(tc.tile_pool(name="stage", bufs=8))
+        stage = ctx.enter_context(tc.tile_pool(name="stage", bufs=7))
         late_p = ctx.enter_context(tc.tile_pool(name="late_p", bufs=1))
+        share0 = ctx.enter_context(tc.tile_pool(name="share0", bufs=1))
+        share1 = ctx.enter_context(tc.tile_pool(name="share1", bufs=1))
         psum = ctx.enter_context(tc.psum_pool(name="psum", bufs=1))
 
         offsets = keep.tile([P, SLOTS // 16], U16, name="offsets")
@@ -48,6 +50,8 @@ def tile_routed_moe_kernel(tc, xT, w, gate, offs, out):
         def load_plane(g, t, pieces=1):
             if g == 1 and t < 2:
                 raw = late_p.tile([P, T], F32, name="late_plane%d" % t, offset=(1 - t) * T * 4)
+            elif g == 1 and t == 2:
+                raw = share0.tile([P, T], F32, name="plane12", offset=0)
             else:
                 raw = stage.tile([P, T], F32, name="raw")
             for c in range(pieces):
@@ -56,18 +60,21 @@ def tile_routed_moe_kernel(tc, xT, w, gate, offs, out):
             planes[(g, t)] = raw
 
         def load_w(b):
-            raw = stage.tile([P, W_BLOCKS, PACK * N], F32, name="raw")
+            if b >= 2:
+                raw = share1.tile([P, W_BLOCKS, PACK * N], F32, name="w_raw%d" % b, offset=(b - 2) * T * 4)
+            else:
+                raw = stage.tile([P, W_BLOCKS, PACK * N], F32, name="raw")
             nc.sync.dma_start(out=raw[:], in_=w_rows[:, b * W_BLOCKS:(b + 1) * W_BLOCKS, :])
             w_raw[b] = raw
 
         load_plane(0, 0)
         load_plane(0, 2, 2)
         load_plane(0, 1)
-        load_plane(0, 3)
+        load_plane(0, 3, 2)
         load_plane(1, 0)
-        load_w(0)
+        load_plane(1, 2, 2)
         load_plane(1, 1)
-        load_plane(1, 2)
+        load_w(0)
         load_plane(1, 3)
         load_w(1)
         nc.sync.dma_start(out=gate_sb[:], in_=gate)
@@ -108,9 +115,13 @@ def tile_routed_moe_kernel(tc, xT, w, gate, offs, out):
         def gather_s(g, t, first, count):
             nc.scalar.activation(out=pair_slice(g, first, count)[:, 1, :, t - 2], in_=xb[:, g, t - 2, :].indirect(slots(first, count)), func=COPY)
 
-        def interleave(g, first, count, pieces=1):
-            whole = keep.tile([P, count, PACK], BF16, name="grouped%d_%d" % (g, first), align_bytes=64)
+        def interleave(g, first, count, pieces=1, engine="V"):
+            if g == 0:
+                whole = share0.tile([P, count, PACK], BF16, name="grouped%d_%d" % (g, first), offset=0, align_bytes=64)
+            else:
+                whole = keep.tile([P, count, PACK], BF16, name="grouped%d_%d" % (g, first), align_bytes=64)
             grouped[g] = (whole, first)
+            grouped[(g, first)] = (whole, first)
             tile_of = pairs[(g, first // span[g])]
             lo = first % span[g]
             words = tile_of[:].rearrange("p u s e -> p (u s e)").bitcast(F32).rearrange("p (u s) -> p u s", u=2)
@@ -119,11 +130,13 @@ def tile_routed_moe_kernel(tc, xT, w, gate, offs, out):
                 step = count // pieces
                 for c in range(pieces):
                     nc.gpsimd.tensor_copy(out=words_out[:, c * step:(c + 1) * step, :], in_=words[:, :, lo + c * step:lo + (c + 1) * step].rearrange("p u s -> p s u"))
+            elif engine == "S":
+                nc.scalar.copy(out=words_out, in_=words[:, :, lo:lo + count].rearrange("p u s -> p s u"))
             else:
                 nc.vector.tensor_copy(out=words_out, in_=words[:, :, lo:lo + count].rearrange("p u s -> p s u"))
 
         def quantize_slots(g, first, count):
-            whole, base = grouped[g]
+            whole, base = grouped.get((g, first), grouped[g])
             nc.vector.quantize_mx(
                 out=x_codes[:, g, first:first + count].bitcast(FP8X4),
                 scales=x_scales[:, g, first:first + count],
@@ -169,7 +182,10 @@ def tile_routed_moe_kernel(tc, xT, w, gate, offs, out):
             acc[b] = bank
 
         def copy_sums(b):
-            y = keep.tile([P, BANK], F32, name="y%d" % b)
+            if b in (1, 2):
+                y = share1.tile([P, BANK], F32, name="y%d" % b, offset=(b - 1) * T * 4)
+            else:
+                y = keep.tile([P, BANK], F32, name="y%d" % b)
             if b == 0:
                 nc.vector.tensor_copy(out=y[:], in_=acc[b][:])
             else:
@@ -188,45 +204,45 @@ def tile_routed_moe_kernel(tc, xT, w, gate, offs, out):
         cast(0, 3, 2, "G")
         for h in range(2):
             gather_s(0, 3, h * HALF, HALF)
-        interleave_w(0, "G")
         for t in range(2):
             for h in range(2):
                 gather_v(1, t, h * HALF, HALF)
         w_scales = late_p.tile([P, BANKS, W_BLOCKS * N], U8, name="w_scales", offset=0, align_bytes=64)
         x_scales = late_p.tile([P, PASSES, SLOTS], U8, name="x_scales", offset=BANKS * W_BLOCKS * N, align_bytes=64)
-        cast(1, 2)
-        cast(1, 3)
+        cast(1, 2, 2, "G")
         interleave(0, 0, SLOTS, 4)
+        gather_s(1, 2, 0, BANK)
+        gather_s(1, 2, BANK, BANK)
+        gather_s(1, 2, HALF, HALF)
+        cast(1, 3)
+        interleave_w(0, "V")
         quantize_w(0)
         quantize_slots(0, 0, HALF)
-        interleave_w(1, "V", W_BLOCKS // 2, W_BLOCKS // 2)
-        gather_s(1, 2, 0, BANK)
         gather_s(1, 3, 0, BANK)
-        interleave_w(1, "S", 0, W_BLOCKS // 2)
         interleave(1, 0, BANK)
-        quantize_slots(0, HALF, HALF)
         quantize_slots(1, 0, BANK)
         multiply(0)
-        gather_s(1, 2, BANK, BANK)
+        quantize_slots(0, HALF, HALF)
+        interleave_w(1, "V", W_BLOCKS // 2, W_BLOCKS // 2)
+        interleave_w(1, "S", 0, W_BLOCKS // 2)
         gather_s(1, 3, BANK, BANK)
         interleave(1, BANK, BANK)
         quantize_w(1)
         quantize_slots(1, BANK, BANK)
         multiply(1)
-        gather_s(1, 2, HALF, HALF)
-        gather_s(1, 3, HALF, HALF)
         copy_sums(0)
-        copy_sums(1)
         scatter(0)
+        gather_s(1, 3, HALF, HALF)
+        interleave(1, 2 * BANK, BANK, 1, "S")
+        interleave(1, 3 * BANK, BANK, 1, "S")
         interleave_w(2, "S")
-        interleave(1, 2 * BANK, BANK)
+        copy_sums(1)
         quantize_w(2)
         quantize_slots(1, 2 * BANK, BANK)
         multiply(2)
         scatter(1)
-        copy_sums(2)
         interleave_w(3, "S")
-        interleave(1, 3 * BANK, BANK)
+        copy_sums(2)
         quantize_w(3)
         quantize_slots(1, 3 * BANK, BANK)
         multiply(3)

@@ -157,11 +157,11 @@ def tile_routed_moe_kernel(tc, xT, w, gate, offs, out):
                 else:
                     nc.scalar.copy(out=runs_out, in_=runs_in)
 
-        def quantize_w(b):
+        def quantize_w(b, first=0, count=W_BLOCKS):
             nc.vector.quantize_mx(
-                out=w_codes[:, b, :].bitcast(FP8X4),
-                scales=w_scales[:, b, :],
-                in_=w_grouped[b][:].rearrange("p x n t -> p (x n t)"),
+                out=w_codes[:, b, first * N:(first + count) * N].bitcast(FP8X4),
+                scales=w_scales[:, b, first * N:(first + count) * N],
+                in_=w_grouped[b][:, first:first + count].rearrange("p x n t -> p (x n t)"),
             )
 
         def multiply(b):
@@ -211,24 +211,24 @@ def tile_routed_moe_kernel(tc, xT, w, gate, offs, out):
         x_scales = late_p.tile([P, PASSES, SLOTS], U8, name="x_scales", offset=BANKS * W_BLOCKS * N, align_bytes=64)
         cast(1, 2, 2, "G")
         interleave(0, 0, SLOTS, 4)
-        gather_s(1, 2, 0, BANK)
-        gather_s(1, 2, BANK, BANK)
+        gather_s(1, 2, 0, HALF)
         gather_s(1, 2, HALF, HALF)
         cast(1, 3)
-        interleave_w(0, "V")
-        quantize_w(0)
+        interleave_w(0, "V", 0, W_BLOCKS // 2)
+        interleave_w(0, "V", W_BLOCKS // 2, W_BLOCKS // 2)
+        quantize_w(0, 0, W_BLOCKS // 2)
+        quantize_w(0, W_BLOCKS // 2, W_BLOCKS // 2)
         quantize_slots(0, 0, HALF)
-        gather_s(1, 3, 0, BANK)
-        interleave(1, 0, BANK)
-        quantize_slots(1, 0, BANK)
-        multiply(0)
+        gather_s(1, 3, 0, HALF)
         quantize_slots(0, HALF, HALF)
         interleave_w(1, "V", W_BLOCKS // 2, W_BLOCKS // 2)
         interleave_w(1, "S", 0, W_BLOCKS // 2)
-        gather_s(1, 3, BANK, BANK)
+        interleave(1, 0, BANK)
         interleave(1, BANK, BANK)
-        quantize_w(1)
+        quantize_slots(1, 0, BANK)
+        multiply(0)
         quantize_slots(1, BANK, BANK)
+        quantize_w(1)
         multiply(1)
         copy_sums(0)
         scatter(0)

@@ -32,7 +32,7 @@ def tile_routed_moe_kernel(tc, xT, w, gate, offs, out):
 
     with ExitStack() as ctx:
         keep = ctx.enter_context(tc.tile_pool(name="keep", bufs=1))
-        stage = ctx.enter_context(tc.tile_pool(name="stage", bufs=7))
+        stage = ctx.enter_context(tc.tile_pool(name="stage", bufs=5))
         late_p = ctx.enter_context(tc.tile_pool(name="late_p", bufs=1))
         share0 = ctx.enter_context(tc.tile_pool(name="share0", bufs=1))
         share1 = ctx.enter_context(tc.tile_pool(name="share1", bufs=1))
@@ -47,10 +47,16 @@ def tile_routed_moe_kernel(tc, xT, w, gate, offs, out):
         sums = {}
         gate_sb = keep.tile([P, SLOTS], F32, name="gate_sb")
 
+        v_planes = late_p.tile([P, 2 * PASSES, T], F32, name="v_planes", offset=0)
+
+        def v_place(g, t):
+            return 2 * PASSES - 1 - (2 * g + t)
+
         def load_plane(g, t, pieces=1):
-            if g == 1 and t < 2:
-                raw = late_p.tile([P, T], F32, name="late_plane%d" % t, offset=(1 - t) * T * 4)
-            elif g == 1 and t == 2:
+            if t < 2:
+                nc.sync.dma_start(out=v_planes[:, v_place(g, t), :], in_=x_planes[g, :, t, :])
+                return
+            if g == 1 and t == 2:
                 raw = share0.tile([P, T], F32, name="plane12", offset=0)
             else:
                 raw = stage.tile([P, T], F32, name="raw")
@@ -86,7 +92,7 @@ def tile_routed_moe_kernel(tc, xT, w, gate, offs, out):
         window = keep.tile([P, T], F32, name="window")
         xb = keep.tile([P, PASSES, 2, T], BF16, name="xb")
 
-        span = (SLOTS, HALF)
+        span = (SLOTS, SLOTS)
         pairs = {}
         grouped = {}
         for g in range(PASSES):
@@ -110,7 +116,10 @@ def tile_routed_moe_kernel(tc, xT, w, gate, offs, out):
             return pairs[(g, first // span[g])][:, :, lo:lo + count, :]
 
         def gather_v(g, t, first, count):
-            nc.vector.tensor_copy(pair_slice(g, first, count)[:, 0, :, t], planes[(g, t)][:].indirect(slots(first, count)))
+            width = 1 if count < SLOTS else 2
+            place = v_place(g, t)
+            view = v_planes[:, place:place + width, :].rearrange("p a n -> p (a n)")
+            nc.vector.tensor_copy(pair_slice(g, first, count)[:, 0, :, t], view.indirect(slots(first, count)))
 
         def gather_s(g, t, first, count):
             nc.scalar.activation(out=pair_slice(g, first, count)[:, 1, :, t - 2], in_=xb[:, g, t - 2, :].indirect(slots(first, count)), func=COPY)
@@ -182,31 +191,37 @@ def tile_routed_moe_kernel(tc, xT, w, gate, offs, out):
             acc[b] = bank
 
         def copy_sums(b):
-            if b in (1, 2):
-                y = share1.tile([P, BANK], F32, name="y%d" % b, offset=(b - 1) * T * 4)
+            if b == 1:
+                y = share1.tile([P, BANK], F32, name="y%d" % b, offset=0)[:]
+            elif b == 2:
+                both = share1.tile([P, 2 * BANK], F32, name="y23", offset=T * 4)
+                sums[23] = both
+                y = both[:, 0:BANK]
+            elif b == 3:
+                y = sums[23][:, BANK:2 * BANK]
             else:
-                y = keep.tile([P, BANK], F32, name="y%d" % b)
+                y = keep.tile([P, BANK], F32, name="y%d" % b)[:]
             if b == 0:
-                nc.vector.tensor_copy(out=y[:], in_=acc[b][:])
+                nc.vector.tensor_copy(out=y, in_=acc[b][:])
             else:
-                nc.scalar.copy(out=y[:], in_=acc[b][:])
+                nc.scalar.copy(out=y, in_=acc[b][:])
             sums[b] = y
 
-        def scatter(b):
-            nc.vector.tensor_tensor(window[:].indirect(slots(b * BANK, BANK)), sums[b][:], gate_sb[:, b * BANK:(b + 1) * BANK], MULT)
+        def scatter(b, banks=1):
+            values = sums[b] if banks == 1 else sums[23][:]
+            nc.vector.tensor_tensor(window[:].indirect(slots(b * BANK, banks * BANK)), values, gate_sb[:, b * BANK:(b + banks) * BANK], MULT)
 
         cast(0, 2, 2)
-        for t in range(2):
-            for h in range(2):
-                gather_v(0, t, h * HALF, HALF)
+        for h in range(2):
+            gather_v(0, 0, h * HALF, HALF)
+        gather_v(0, 1, 0, SLOTS)
         for h in range(2):
             gather_s(0, 2, h * HALF, HALF)
         cast(0, 3, 2, "G")
         for h in range(2):
             gather_s(0, 3, h * HALF, HALF)
         for t in range(2):
-            for h in range(2):
-                gather_v(1, t, h * HALF, HALF)
+            gather_v(1, t, 0, SLOTS)
         w_scales = late_p.tile([P, BANKS, W_BLOCKS * N], U8, name="w_scales", offset=0, align_bytes=64)
         x_scales = late_p.tile([P, PASSES, SLOTS], U8, name="x_scales", offset=BANKS * W_BLOCKS * N, align_bytes=64)
         cast(1, 2, 2, "G")
@@ -233,20 +248,17 @@ def tile_routed_moe_kernel(tc, xT, w, gate, offs, out):
         copy_sums(0)
         scatter(0)
         gather_s(1, 3, HALF, HALF)
-        interleave(1, 2 * BANK, BANK, 1, "S")
-        interleave(1, 3 * BANK, BANK, 1, "S")
+        interleave(1, HALF, HALF, 1, "S")
         interleave_w(2, "S")
         copy_sums(1)
+        quantize_slots(1, HALF, HALF)
         quantize_w(2)
-        quantize_slots(1, 2 * BANK, BANK)
         multiply(2)
         scatter(1)
         interleave_w(3, "S")
         copy_sums(2)
         quantize_w(3)
-        quantize_slots(1, 3 * BANK, BANK)
         multiply(3)
         copy_sums(3)
-        scatter(2)
-        scatter(3)
+        scatter(2, 2)
         nc.sync.dma_start(out=out, in_=window[:])

@@ -192,7 +192,7 @@ def tile_routed_moe_kernel(tc, xT, w, gate, offs, out):
 
         def copy_sums(b):
             if b == 1:
-                y = share1.tile([P, BANK], F32, name="y%d" % b, offset=0)[:]
+                y = share1.tile([P, BANK], F32, name="y%d" % b, offset=T * 4 + 2 * BANK * 4)[:]
             elif b == 2:
                 both = share1.tile([P, 2 * BANK], F32, name="y23", offset=T * 4)
                 sums[23] = both
@@ -236,8 +236,7 @@ def tile_routed_moe_kernel(tc, xT, w, gate, offs, out):
         quantize_slots(0, 0, HALF)
         gather_s(1, 3, 0, HALF)
         quantize_slots(0, HALF, HALF)
-        interleave_w(1, "V", W_BLOCKS // 2, W_BLOCKS // 2)
-        interleave_w(1, "S", 0, W_BLOCKS // 2)
+        interleave_w(1, "V")
         interleave(1, 0, BANK)
         interleave(1, BANK, BANK)
         quantize_slots(1, 0, BANK)
@@ -250,15 +249,15 @@ def tile_routed_moe_kernel(tc, xT, w, gate, offs, out):
         gather_s(1, 3, HALF, HALF)
         interleave(1, HALF, HALF, 1, "S")
         interleave_w(2, "S")
-        copy_sums(1)
         quantize_slots(1, HALF, HALF)
         quantize_w(2)
         multiply(2)
-        scatter(1)
         interleave_w(3, "S")
-        copy_sums(2)
+        copy_sums(1)
         quantize_w(3)
         multiply(3)
+        scatter(1)
+        copy_sums(2)
         copy_sums(3)
         scatter(2, 2)
         nc.sync.dma_start(out=out, in_=window[:])

@@ -191,25 +191,18 @@ def tile_routed_moe_kernel(tc, xT, w, gate, offs, out):
             acc[b] = bank
 
         def copy_sums(b):
-            if b == 1:
-                y = share1.tile([P, BANK], F32, name="y%d" % b, offset=T * 4 + 2 * BANK * 4)[:]
-            elif b == 2:
-                both = share1.tile([P, 2 * BANK], F32, name="y23", offset=T * 4)
-                sums[23] = both
-                y = both[:, 0:BANK]
-            elif b == 3:
-                y = sums[23][:, BANK:2 * BANK]
+            if b in (1, 2):
+                y = share1.tile([P, BANK], F32, name="y%d" % b, offset=(b - 1) * T * 4)
             else:
-                y = keep.tile([P, BANK], F32, name="y%d" % b)[:]
+                y = keep.tile([P, BANK], F32, name="y%d" % b)
             if b == 0:
-                nc.vector.tensor_copy(out=y, in_=acc[b][:])
+                nc.vector.tensor_copy(out=y[:], in_=acc[b][:])
             else:
-                nc.scalar.copy(out=y, in_=acc[b][:])
+                nc.scalar.copy(out=y[:], in_=acc[b][:])
             sums[b] = y
 
-        def scatter(b, banks=1):
-            values = sums[b] if banks == 1 else sums[23][:]
-            nc.vector.tensor_tensor(window[:].indirect(slots(b * BANK, banks * BANK)), values, gate_sb[:, b * BANK:(b + banks) * BANK], MULT)
+        def scatter(b):
+            nc.vector.tensor_tensor(window[:].indirect(slots(b * BANK, BANK)), sums[b][:], gate_sb[:, b * BANK:(b + 1) * BANK], MULT)
 
         cast(0, 2, 2)
         for h in range(2):
@@ -237,27 +230,31 @@ def tile_routed_moe_kernel(tc, xT, w, gate, offs, out):
         gather_s(1, 3, 0, HALF)
         quantize_slots(0, HALF, HALF)
         interleave_w(1, "V")
-        interleave(1, 0, BANK)
-        interleave(1, BANK, BANK)
+        interleave(1, 0, BANK, 1, "S")
+        interleave(1, BANK, BANK, 1, "S")
         quantize_slots(1, 0, BANK)
         multiply(0)
-        quantize_slots(1, BANK, BANK)
         quantize_w(1)
+        quantize_slots(1, BANK, BANK)
         multiply(1)
         copy_sums(0)
         scatter(0)
-        gather_s(1, 3, HALF, HALF)
-        interleave(1, HALF, HALF, 1, "S")
+        gather_s(1, 3, 2 * BANK, BANK)
+        interleave(1, 2 * BANK, BANK, 1, "S")
         interleave_w(2, "S")
-        quantize_slots(1, HALF, HALF)
+        copy_sums(1)
+        quantize_slots(1, 2 * BANK, BANK)
         quantize_w(2)
         multiply(2)
+        scatter(1)
+        gather_s(1, 3, 3 * BANK, BANK)
+        interleave(1, 3 * BANK, BANK, 1, "S")
         interleave_w(3, "S")
-        copy_sums(1)
+        copy_sums(2)
+        quantize_slots(1, 3 * BANK, BANK)
         quantize_w(3)
         multiply(3)
-        scatter(1)
-        copy_sums(2)
+        scatter(2)
         copy_sums(3)
-        scatter(2, 2)
+        scatter(3)
         nc.sync.dma_start(out=out, in_=window[:])

@@ -32,7 +32,7 @@ def tile_routed_moe_kernel(tc, xT, w, gate, offs, out):
 
     with ExitStack() as ctx:
         keep = ctx.enter_context(tc.tile_pool(name="keep", bufs=1))
-        stage = ctx.enter_context(tc.tile_pool(name="stage", bufs=5))
+        stage = ctx.enter_context(tc.tile_pool(name="stage", bufs=4))
         late_p = ctx.enter_context(tc.tile_pool(name="late_p", bufs=1))
         share0 = ctx.enter_context(tc.tile_pool(name="share0", bufs=1))
         share1 = ctx.enter_context(tc.tile_pool(name="share1", bufs=1))
@@ -47,7 +47,7 @@ def tile_routed_moe_kernel(tc, xT, w, gate, offs, out):
         sums = {}
         gate_sb = keep.tile([P, SLOTS], F32, name="gate_sb")
 
-        v_planes = late_p.tile([P, 2 * PASSES, T], F32, name="v_planes", offset=0)
+        v_planes = late_p.tile([P, 2 * PASSES + 1, T], F32, name="v_planes", offset=0)
 
         def v_place(g, t):
             return 2 * PASSES - 1 - (2 * g + t)
@@ -82,8 +82,8 @@ def tile_routed_moe_kernel(tc, xT, w, gate, offs, out):
         load_plane(1, 1)
         load_w(0)
         load_plane(1, 3)
-        load_w(1)
         nc.sync.dma_start(out=gate_sb[:], in_=gate)
+        load_w(1)
         load_w(2)
         load_w(3)
 
@@ -205,8 +205,7 @@ def tile_routed_moe_kernel(tc, xT, w, gate, offs, out):
             nc.vector.tensor_tensor(window[:].indirect(slots(b * BANK, BANK)), sums[b][:], gate_sb[:, b * BANK:(b + 1) * BANK], MULT)
 
         cast(0, 2, 2)
-        for h in range(2):
-            gather_v(0, 0, h * HALF, HALF)
+        gather_v(0, 0, 0, SLOTS)
         gather_v(0, 1, 0, SLOTS)
         for h in range(2):
             gather_s(0, 2, h * HALF, HALF)
@@ -222,10 +221,8 @@ def tile_routed_moe_kernel(tc, xT, w, gate, offs, out):
         gather_s(1, 2, 0, HALF)
         gather_s(1, 2, HALF, HALF)
         cast(1, 3)
-        interleave_w(0, "V", 0, W_BLOCKS // 2)
-        interleave_w(0, "V", W_BLOCKS // 2, W_BLOCKS // 2)
-        quantize_w(0, 0, W_BLOCKS // 2)
-        quantize_w(0, W_BLOCKS // 2, W_BLOCKS // 2)
+        interleave_w(0, "G")
+        quantize_w(0)
         quantize_slots(0, 0, HALF)
         gather_s(1, 3, 0, HALF)
         quantize_slots(0, HALF, HALF)

from contextlib import ExitStack

import concourse.mybir as mybir

K, T, E, C, N = 1024, 2048, 8, 256, 128
FLOPS = 2 * K * N * E * C

F32 = mybir.dt.float32
BF16 = mybir.dt.bfloat16
U32 = mybir.dt.uint32
U16 = mybir.dt.uint16
U8 = mybir.dt.uint8
FP8X4 = mybir.dt.float8_e4m3fn_x4
MULT = mybir.AluOpType.mult
COPY = mybir.ActivationFunctionType.Copy

P = 128
PACK = 4
PASSES = K // (P * PACK)
SLOTS = E * C
HALF = SLOTS // 2
BANK = 512
BANKS = SLOTS // BANK
W_BLOCKS = E * PASSES // BANKS
RUN = 4


def tile_routed_moe_kernel(tc, xT, w, gate, offs, out):
    nc = tc.nc
    x_planes = xT.rearrange("(g p t) n -> g p t n", g=PASSES, p=P, t=PACK)
    w_rows = w.rearrange("e (g p t) n -> p (e g) (t n)", g=PASSES, p=P, t=PACK)

    with ExitStack() as ctx:
        keep = ctx.enter_context(tc.tile_pool(name="keep", bufs=1))
        stage = ctx.enter_context(tc.tile_pool(name="stage", bufs=4))
        late_p = ctx.enter_context(tc.tile_pool(name="late_p", bufs=1))
        share0 = ctx.enter_context(tc.tile_pool(name="share0", bufs=1))
        share1 = ctx.enter_context(tc.tile_pool(name="share1", bufs=1))
        psum = ctx.enter_context(tc.psum_pool(name="psum", bufs=1))

        offsets = keep.tile([P, SLOTS // 16], U16, name="offsets")
        nc.sync.dma_start(offsets[:], offs)

        planes = {}
        w_raw = {}
        acc = {}
        sums = {}
        gate_sb = keep.tile([P, SLOTS], F32, name="gate_sb")

        v_planes = late_p.tile([P, 2 * PASSES + 1, T], F32, name="v_planes", offset=0)

        def v_place(g, t):
            return 2 * PASSES - 1 - (2 * g + t)

        def load_plane(g, t, pieces=1):
            if t < 2:
                nc.sync.dma_start(out=v_planes[:, v_place(g, t), :], in_=x_planes[g, :, t, :])
                return
            if g == 1 and t == 2:
                raw = share0.tile([P, T], F32, name="plane12", offset=0)
            else:
                raw = stage.tile([P, T], F32, name="raw")
            for c in range(pieces):
                cols = slice(c * T // pieces, (c + 1) * T // pieces)
                nc.sync.dma_start(out=raw[:, cols], in_=x_planes[g, :, t, cols])
            planes[(g, t)] = raw

        def load_w(b):
            if b >= 2:
                raw = share1.tile([P, W_BLOCKS, PACK * N], F32, name="w_raw%d" % b, offset=(b - 2) * T * 4)
            else:
                raw = stage.tile([P, W_BLOCKS, PACK * N], F32, name="raw")
            nc.sync.dma_start(out=raw[:], in_=w_rows[:, b * W_BLOCKS:(b + 1) * W_BLOCKS, :])
            w_raw[b] = raw

        load_plane(0, 0)
        load_plane(0, 2, 2)
        load_plane(0, 1)
        load_plane(0, 3, 2)
        load_plane(1, 0)
        load_plane(1, 2, 2)
        load_plane(1, 1)
        load_w(0)
        load_plane(1, 3)
        nc.sync.dma_start(out=gate_sb[:], in_=gate)
        load_w(1)
        load_w(2)
        load_w(3)

        x_codes = keep.tile([P, PASSES, SLOTS], U32, name="x_codes", align_bytes=64)
        w_codes = keep.tile([P, BANKS, W_BLOCKS * N], U32, name="w_codes", align_bytes=64)
        window = keep.tile([P, T], F32, name="window")
        xb = keep.tile([P, PASSES, 2, T], BF16, name="xb")

        span = (SLOTS, SLOTS)
        pairs = {}
        grouped = {}
        for g in range(PASSES):
            for c in range(SLOTS // span[g]):
                pairs[(g, c)] = keep.tile([P, 2, span[g], 2], BF16, name="pairs%d_%d" % (g, c), align_bytes=64)
        w_grouped = [keep.tile([P, W_BLOCKS, N, PACK], BF16, name="w_grouped%d" % b, align_bytes=64) for b in range(BANKS)]

        def slots(first, count):
            return offsets[:, first // 16:(first + count) // 16]

        def cast(g, t, pieces=1, engine="S"):
            for c in range(pieces):
                cols = slice(c * T // pieces, (c + 1) * T // pieces)
                if engine == "G":
                    nc.gpsimd.tensor_copy(out=xb[:, g, t - 2, cols], in_=planes[(g, t)][:, cols])
                else:
                    nc.scalar.copy(out=xb[:, g, t - 2, cols], in_=planes[(g, t)][:, cols])

        def pair_slice(g, first, count):
            lo = first % span[g]
            return pairs[(g, first // span[g])][:, :, lo:lo + count, :]

        def gather_v(g, t, first, count):
            width = 1 if count < SLOTS else 2
            place = v_place(g, t)
            view = v_planes[:, place:place + width, :].rearrange("p a n -> p (a n)")
            nc.vector.tensor_copy(pair_slice(g, first, count)[:, 0, :, t], view.indirect(slots(first, count)))

        def gather_s(g, t, first, count):
            nc.scalar.activation(out=pair_slice(g, first, count)[:, 1, :, t - 2], in_=xb[:, g, t - 2, :].indirect(slots(first, count)), func=COPY)

        def interleave(g, first, count, pieces=1, engine="V"):
            if g == 0:
                whole = share0.tile([P, count, PACK], BF16, name="grouped%d_%d" % (g, first), offset=0, align_bytes=64)
            else:
                whole = keep.tile([P, count, PACK], BF16, name="grouped%d_%d" % (g, first), align_bytes=64)
            grouped[g] = (whole, first)
            grouped[(g, first)] = (whole, first)
            tile_of = pairs[(g, first // span[g])]
            lo = first % span[g]
            words = tile_of[:].rearrange("p u s e -> p (u s e)").bitcast(F32).rearrange("p (u s) -> p u s", u=2)
            words_out = whole[:].rearrange("p s t -> p (s t)").bitcast(F32).rearrange("p (s u) -> p s u", u=2)
            if g == 0:
                step = count // pieces
                for c in range(pieces):
                    nc.gpsimd.tensor_copy(out=words_out[:, c * step:(c + 1) * step, :], in_=words[:, :, lo + c * step:lo + (c + 1) * step].rearrange("p u s -> p s u"))
            elif engine == "S":
                nc.scalar.copy(out=words_out, in_=words[:, :, lo:lo + count].rearrange("p u s -> p s u"))
            else:
                nc.vector.tensor_copy(out=words_out, in_=words[:, :, lo:lo + count].rearrange("p u s -> p s u"))

        def quantize_slots(g, first, count):
            whole, base = grouped.get((g, first), grouped[g])
            nc.vector.quantize_mx(
                out=x_codes[:, g, first:first + count].bitcast(FP8X4),
                scales=x_scales[:, g, first:first + count],
                in_=whole[:, first - base:first - base + count, :].rearrange("p s t -> p (s t)"),
            )

        def interleave_w(b, engine, first=0, count=W_BLOCKS):
            dst = w_grouped[b]
            if engine == "G":
                src = w_raw[b][:].rearrange("p x (t n) -> p x n t", t=PACK)
                for x in range(W_BLOCKS):
                    nc.gpsimd.tensor_copy(out=dst[:, x:x + 1], in_=src[:, x:x + 1])
            else:
                runs_in = w_raw[b][:, first:first + count, :].rearrange("p x (t c i) -> p x c t i", t=PACK, i=RUN)
                runs_out = dst[:, first:first + count].rearrange("p x (c i) t -> p x c t i", i=RUN)
                if engine == "V":
                    nc.vector.tensor_copy(out=runs_out, in_=runs_in)
                else:
                    nc.scalar.copy(out=runs_out, in_=runs_in)

        def quantize_w(b, first=0, count=W_BLOCKS):
            nc.vector.quantize_mx(
                out=w_codes[:, b, first * N:(first + count) * N].bitcast(FP8X4),
                scales=w_scales[:, b, first * N:(first + count) * N],
                in_=w_grouped[b][:, first:first + count].rearrange("p x n t -> p (x n t)"),
            )

        def multiply(b):
            bank = psum.tile([P, BANK], F32, name="acc%d" % b)
            for j in range(BANK // C):
                e = b * BANK // C + j
                for g in range(PASSES):
                    x = j * PASSES + g
                    nc.tensor.matmul_mx(
                        out=bank[:, j * C:(j + 1) * C],
                        lhsT=w_codes[:, b, x * N:(x + 1) * N].bitcast(FP8X4),
                        lhsT_scale=w_scales[:, b, x * N:(x + 1) * N],
                        rhs=x_codes[:, g, e * C:(e + 1) * C].bitcast(FP8X4),
                        rhs_scale=x_scales[:, g, e * C:(e + 1) * C],
                        start=(g == 0),
                        stop=(g == PASSES - 1),
                    )
            acc[b] = bank

        def copy_sums(b):
            if b in (1, 2):
                y = share1.tile([P, BANK], F32, name="y%d" % b, offset=(b - 1) * T * 4)
            else:
                y = keep.tile([P, BANK], F32, name="y%d" % b)
            if b == 0:
                nc.vector.tensor_copy(out=y[:], in_=acc[b][:])
            else:
                nc.scalar.copy(out=y[:], in_=acc[b][:])
            sums[b] = y

        def scatter(b):
            nc.vector.tensor_tensor(window[:].indirect(slots(b * BANK, BANK)), sums[b][:], gate_sb[:, b * BANK:(b + 1) * BANK], MULT)

        cast(0, 2, 2)
        gather_v(0, 0, 0, SLOTS)
        gather_v(0, 1, 0, SLOTS)
        for h in range(2):
            gather_s(0, 2, h * HALF, HALF)
        cast(0, 3, 2, "G")
        for h in range(2):
            gather_s(0, 3, h * HALF, HALF)
        for t in range(2):
            gather_v(1, t, 0, SLOTS)
        w_scales = late_p.tile([P, BANKS, W_BLOCKS * N], U8, name="w_scales", offset=0, align_bytes=64)
        x_scales = late_p.tile([P, PASSES, SLOTS], U8, name="x_scales", offset=BANKS * W_BLOCKS * N, align_bytes=64)
        cast(1, 2, 2, "G")
        interleave(0, 0, SLOTS, 4)
        gather_s(1, 2, 0, HALF)
        gather_s(1, 2, HALF, HALF)
        cast(1, 3)
        interleave_w(0, "G")
        quantize_w(0)
        quantize_slots(0, 0, HALF)
        gather_s(1, 3, 0, HALF)
        quantize_slots(0, HALF, HALF)
        interleave_w(1, "V")
        interleave(1, 0, BANK, 1, "S")
        interleave(1, BANK, BANK, 1, "S")
        quantize_slots(1, 0, BANK)
        multiply(0)
        quantize_w(1)
        quantize_slots(1, BANK, BANK)
        multiply(1)
        copy_sums(0)
        scatter(0)
        gather_s(1, 3, 2 * BANK, BANK)
        interleave(1, 2 * BANK, BANK, 1, "S")
        interleave_w(2, "S")
        copy_sums(1)
        quantize_slots(1, 2 * BANK, BANK)
        quantize_w(2)
        multiply(2)
        scatter(1)
        gather_s(1, 3, 3 * BANK, BANK)
        interleave(1, 3 * BANK, BANK, 1, "S")
        interleave_w(3, "S")
        copy_sums(2)
        quantize_slots(1, 3 * BANK, BANK)
        quantize_w(3)
        multiply(3)
        scatter(2)
        copy_sums(3)
        scatter(3)
        nc.sync.dma_start(out=out, in_=window[:])
